import numpy as np
import ml_dtypes


def mxq(x, axis, fmt="e4m3"):
    dtype, down = {"e4m3": (ml_dtypes.float8_e4m3fn, 7), "e5m2": (ml_dtypes.float8_e5m2, 14)}[fmt]
    v = np.moveaxis(np.asarray(x, np.float32).astype(ml_dtypes.bfloat16).astype(np.float64), axis, -1)
    blocks = v.reshape(v.shape[:-1] + (-1, 32))
    amax = np.abs(blocks).max(-1, keepdims=True)
    byte = np.maximum(np.where(amax > 0, np.frexp(amax)[1] - 1 + 127, 0) - down, 1)
    scale = np.exp2(byte - 127.0)
    codes = (blocks / scale).astype(np.float32).astype(dtype).astype(np.float64)
    return np.moveaxis((codes * scale).reshape(v.shape), -1, axis)


WIDE = False


def mx_kscale(k):
    if not WIDE:
        return np.ones(k)
    levels = np.array([10, -10, 5, -5, 0])
    if k % 512:
        return np.exp2(np.random.permutation(np.resize(levels, k // 32))).repeat(32)
    a = np.empty((k // 512, 16))
    for p in range(k // 512):
        a[p, :8] = np.random.permutation(np.resize(levels, 8))
        for g in range(8):
            far = levels[np.abs(levels - a[p, g]) >= 10]
            a[p, g + 8] = far[np.random.randint(len(far))]
    return np.exp2(a.ravel()).repeat(32)


def f64(x):
    return np.asarray(x).astype(np.float64)


def striped(idx):
    return np.tile(idx.reshape(-1, 16).T, (8, 1)).astype(np.uint16)


def unstriped(offs):
    return offs[:16].T.reshape(-1).astype(np.int64)


E2M1 = np.array([0.0, 0.5, 1.0, 1.5, 2.0, 3.0, 4.0, 6.0, -0.0, -0.5, -1.0, -1.5, -2.0, -3.0, -4.0, -6.0])


def pack_weight(w, fmt):
    k, n = w.shape
    w = f64(np.asarray(w, np.float32).astype(ml_dtypes.bfloat16)).reshape(k // 32, 32, n)
    amax = np.abs(w).max(1)
    if fmt == "e4m3":
        byte = np.frexp(amax)[1] - 1 + 127 - 7
    else:
        mant, ex = np.frexp(amax / 6.0)
        byte = np.where(mant > 0.5, ex, ex - 1) + 127
    byte = np.clip(np.where(amax > 0, byte, 1), 1, 254)
    scaled = (w * np.exp2(127.0 - byte)[:, None, :]).reshape(k, n).astype(np.float32)
    by_word = np.ascontiguousarray(scaled.reshape(k // 512, 128, 4, n).transpose(0, 1, 3, 2))
    if fmt == "e4m3":
        words = by_word.astype(ml_dtypes.float8_e4m3fn).view(np.uint8)
    else:
        c = by_word.astype(ml_dtypes.float4_e2m1fn).view(np.uint8) & 0xF
        words = (c[..., 0::2] | (c[..., 1::2] << 4)).reshape(k // 512, 128, 2 * n)
    return np.ascontiguousarray(words), np.ascontiguousarray(byte.astype(np.uint8).reshape(k // 512, 16, n))


def unpack_weight(words, scales, fmt):
    g, _, n = scales.shape
    words = np.ascontiguousarray(words).reshape(g, 128, n, -1)
    if fmt == "e4m3":
        vals = words.view(ml_dtypes.float8_e4m3fn).astype(np.float64)
    else:
        nib = np.empty((g, 128, n, 4), np.uint8)
        nib[..., 0::2] = words & 0xF
        nib[..., 1::2] = words >> 4
        vals = E2M1[nib]
    vals = vals * np.repeat(np.exp2(scales.astype(np.float64) - 127.0), 8, axis=1)[..., None]
    return vals.transpose(0, 1, 3, 2).reshape(g * 512, n)


def gelu(v):
    return 0.5 * v * (1.0 + np.tanh(np.sqrt(2.0 / np.pi) * (v + 0.044715 * v**3)))


def striped8(idx):
    return np.concatenate([v.reshape(-1, 16).T for v in idx]).astype(np.uint16)


def unstriped8(offs):
    return np.stack([offs[16 * g:16 * g + 16].T.reshape(-1) for g in range(8)]).astype(np.int64)


def runs(v, idx8):
    k = np.arange(v.shape[0])
    return v[k[:, None], idx8[k % 512 // 64]]


def often(T, S):
    return np.random.permutation(T)[(T * np.random.uniform(0, 1, S) ** 4).astype(np.int64)]


K, T, S, H, N = 1024, 2048, 1024, 1024, 512

def setup_inputs():
    n = np.random.standard_normal
    s = mx_kscale(K)[:, None]
    u = mx_kscale(H)[:, None]
    tab_words, tab_scales = pack_weight(n((K, T)) * s, "e4m3")
    offs = striped8(np.stack([often(T, S) for _ in range(8)]))
    w1 = (1.5 * n((K, H)) / np.sqrt(K) / s).astype(np.float32)
    w4_words, w4_scales = pack_weight(1.5 * n((K, N)) / np.sqrt(K) / s, "e2m1")
    gain = (np.exp(0.3 * n(H)) * u[:, 0]).astype(np.float32)
    w3 = (1.5 * n((H, N)) / np.sqrt(H) / u).astype(np.float32)
    bg = (0.5 * n(N)).astype(np.float32)
    return {"tab_words": tab_words, "tab_scales": tab_scales, "offs": offs,
            "w1": w1, "w4_words": w4_words, "w4_scales": w4_scales,
            "gain": gain, "w3": w3, "bg": bg}

def reference(tab_words, tab_scales, offs, w1, w4_words, w4_scales, gain, w3, bg):
    v = runs(unpack_weight(tab_words, tab_scales, "e4m3"), unstriped8(offs))
    w4 = unpack_weight(w4_words, w4_scales, "e2m1")
    a = mxq(f64(w1), 0, "e4m3").T @ v
    h = a / (1.0 + np.exp(-a)) * f64(gain)[:, None]
    b = (w4.T @ v) + f64(bg)[:, None]
    y = mxq(f64(w3), 0, "e4m3").T @ mxq(h, 0, "e4m3")
    return y * (1.0 / (1.0 + np.exp(-b)))

@@ -1,0 +1,226 @@
+from contextlib import ExitStack
+
+import concourse.mybir as mybir
+
+K, T, S, H, N = 1024, 2048, 1024, 1024, 512
+FLOPS = 2 * S * (K * H + K * N + H * N)
+
+F32 = mybir.dt.float32
+BF16 = mybir.dt.bfloat16
+I32 = mybir.dt.int32
+U32 = mybir.dt.uint32
+U16 = mybir.dt.uint16
+U8 = mybir.dt.uint8
+FP8X4 = mybir.dt.float8_e4m3fn_x4
+FP4X4 = mybir.dt.float4_e2m1fn_x4
+ACT = mybir.ActivationFunctionType
+ALU = mybir.AluOpType
+
+P = 128
+PACK = 4
+KP = P * PACK
+HALF = 512
+CHUNK = 256
+BANK_TOK = 128
+
+
+def tile_list_premise_slot_gate_kernel(tc, tab_words, tab_scales, offs, w1, w4_words, w4_scales, gain, w3, bg, out):
+    nc = tc.nc
+    with ExitStack() as ctx:
+        keep = ctx.enter_context(tc.tile_pool(name="keep", bufs=1))
+        stage = ctx.enter_context(tc.tile_pool(name="stage", bufs=1))
+        ring = ctx.enter_context(tc.tile_pool(name="ring", bufs=3))
+        work = ctx.enter_context(tc.tile_pool(name="work", bufs=3))
+        psum_a = ctx.enter_context(tc.psum_pool(name="psum_a", bufs=4))
+        psum_o = ctx.enter_context(tc.psum_pool(name="psum_o", bufs=4))
+
+        offsets = keep.tile([P, S // 16], U16, name="offsets")
+        nc.sync.dma_start(offsets[:], offs)
+
+        swin = ring.tile([P, T], U8, name="swin", tag="big", align_bytes=64)
+        swin32 = swin[:].bitcast(I32)
+        nc.gpsimd.memset(swin32, 0)
+        ts32 = tab_scales.bitcast(I32)
+        for a in range(2):
+            for e in range(2):
+                nc.sync.dma_start(swin32[2 * a + e : P : 16, :], ts32[a, e:16:2, :])
+
+        bg_sb = keep.tile([P, 4], F32, name="bg_sb")
+        with nc.allow_non_contiguous_dma(reason="one bias value a partition"):
+            nc.gpsimd.dma_start(bg_sb[:], bg.rearrange("(c p) -> p c", p=P))
+        gain_sb = keep.tile([P, 2, PACK], F32, name="gain_sb")
+        nc.sync.dma_start(gain_sb[:], gain.rearrange("(b p t) -> p b t", p=P, t=PACK))
+
+        tabs = []
+
+        def load_tab(a):
+            tab = ring.tile([P, T], U32, name="tab%d" % a, tag="big", align_bytes=64)
+            nc.sync.dma_start(tab[:].bitcast(I32), tab_words[a].rearrange("p t i -> p (t i)").bitcast(I32))
+            tabs.append(tab)
+
+        w4c = keep.tile([P, 2, 2 * N], U8, name="w4c", align_bytes=64)
+        nc.sync.dma_start(w4c[:].bitcast(I32), w4_words.bitcast(I32).rearrange("a p n -> p a n"))
+        load_tab(0)
+        w4s = keep.tile([P, 2, N], U8, name="w4s", align_bytes=64)
+        nc.vector.memset(w4s[:].bitcast(I32), 0)
+        w4s_src = w4_scales.bitcast(I32).rearrange("a q n -> q a n")
+        for d in range(4):
+            nc.sync.dma_start(w4s[:].bitcast(I32)[32 * d : 32 * d + 4], w4s_src[4 * d : 4 * d + 4])
+        load_tab(1)
+
+        vs = [keep.tile([P, S], U8, name="vs%d" % a, align_bytes=64) for a in range(2)]
+        nc.vector.memset(vs[1][:].bitcast(I32), 0)
+        warm = keep.tile([P, 2], F32, name="warm")
+        nc.vector.memset(warm[:, 0:1], 0.0)
+        nc.scalar.activation(warm[:, 1:2], warm[:, 0:1], ACT.Silu)
+
+        sg = keep.tile([P, S], U8, name="sg", align_bytes=64)
+        nc.vector.tensor_copy(sg[:], swin[:].indirect(offsets[:]))
+        sg32 = sg[:].bitcast(I32)
+        nc.vector.tensor_copy(vs[0][:].bitcast(I32), sg32)
+        for r in range(4):
+            nc.sync.dma_start(vs[1][:].bitcast(I32)[r:P:32, :], sg32[16 * (r // 2) + 2 + r % 2 : P : 32, :])
+        for e in range(2):
+            nc.sync.dma_start(vs[0][:].bitcast(I32)[2 + e : P : 32, :], sg32[16 + e : P : 32, :])
+
+        vw = {}
+        for a in range(2):
+            for h in range(2):
+                g = keep.tile([P, HALF], U32, name="vw%d%d" % (a, h), align_bytes=64)
+                nc.vector.tensor_copy(g[:], tabs[a][:].indirect(offsets[:, 32 * h : 32 * h + 32]))
+                vw[a, h] = g
+
+        half_bg = keep.tile([P, 4], F32, name="half_bg")
+        nc.gpsimd.tensor_scalar(half_bg[:], bg_sb[:], 0.5, 0.0, ALU.mult, ALU.add)
+        half_gain = keep.tile([P, 2, PACK], F32, name="half_gain")
+        nc.gpsimd.tensor_scalar(half_gain[:], gain_sb[:], 0.5, 0.0, ALU.mult, ALU.add)
+
+        def quantize(codes, scales, src):
+            nc.vector.quantize_mx(out=codes.bitcast(FP8X4), scales=scales, in_=src)
+
+        def copy_on(engine, dst, src):
+            if engine == "v":
+                nc.vector.tensor_copy(dst, src)
+            else:
+                nc.scalar.copy(dst, src)
+
+        w1c, w1s = {}, {}
+
+        def load_w1(a, b, engine, pieces):
+            raw = ring.tile([P, PACK, KP], F32, name="raw1", tag="big", align_bytes=64)
+            nc.sync.dma_start(raw[:], w1[KP * a : KP * (a + 1), KP * b : KP * (b + 1)].rearrange("(p j) c -> p j c", j=PACK))
+            grp = stage.tile([P, PACK, P, PACK], BF16, name="grp", align_bytes=64)
+            step = P // pieces
+            for m0 in range(0, P, step):
+                copy_on(
+                    engine,
+                    grp[:, :, m0 : m0 + step, :].rearrange("p t m j -> p m j t"),
+                    raw[:].rearrange("p j (m t) -> p m j t", t=PACK)[:, m0 : m0 + step],
+                )
+            w1c[a, b] = keep.tile([P, KP], U32, name="w1c%d%d" % (a, b), align_bytes=64)
+            w1s[a, b] = keep.tile([P, KP], U8, name="w1s%d%d" % (a, b), align_bytes=64)
+            quantize(w1c[a, b][:], w1s[a, b][:], grp[:].rearrange("p t m j -> p (t m j)"))
+
+        w3c, w3s = {}, {}
+
+        def load_w3(b, engine, pieces):
+            raw = ring.tile([P, PACK, N], F32, name="raw3", tag="big", align_bytes=64)
+            nc.sync.dma_start(raw[:], w3[KP * b : KP * (b + 1), :].rearrange("(p j) n -> p j n", j=PACK))
+            grp = stage.tile([P, N, PACK], BF16, name="grp", align_bytes=64)
+            step = (N // 4) // pieces
+            for c0 in range(0, N // 4, step):
+                copy_on(
+                    engine,
+                    grp[:].rearrange("p (c i) j -> p c j i", i=4)[:, c0 : c0 + step],
+                    raw[:].rearrange("p j (c i) -> p c j i", i=4)[:, c0 : c0 + step],
+                )
+            w3c[b] = keep.tile([P, N], U32, name="w3c%d" % b, align_bytes=64)
+            w3s[b] = keep.tile([P, N], U8, name="w3s%d" % b, align_bytes=64)
+            quantize(w3c[b][:], w3s[b][:], grp[:].rearrange("p n j -> p (n j)"))
+
+        th = keep.tile([P, 4, S], F32, name="th")
+
+        def gate(h):
+            cols = slice(HALF * h, HALF * (h + 1))
+            for c in range(4):
+                acc = psum_o.tile([P, HALF], F32, name="acc_o")
+                for a in range(2):
+                    nc.tensor.matmul_mx(
+                        out=acc[:],
+                        lhsT=w4c[:, a, 2 * P * c : 2 * P * (c + 1)].bitcast(FP4X4),
+                        lhsT_scale=w4s[:, a, P * c : P * (c + 1)],
+                        rhs=vw[a, h][:].bitcast(FP8X4),
+                        rhs_scale=vs[a][:, cols],
+                        start=(a == 0),
+                        stop=(a == 1),
+                    )
+                nc.scalar.activation(th[:, c, cols], acc[:], ACT.Tanh, bias=half_bg[:, c : c + 1], scale=0.5)
+
+        hc, hs = {}, {}
+
+        def hidden(b, u):
+            act = work.tile([P, CHUNK, PACK], F32, name="act")
+            for s in range(CHUNK // BANK_TOK):
+                j0 = CHUNK * u + BANK_TOK * s
+                h, loc = divmod(j0, HALF)
+                acc = psum_a.tile([P, PACK, BANK_TOK], F32, name="acc_a")
+                for t in range(PACK):
+                    for a in range(2):
+                        nc.tensor.matmul_mx(
+                            out=acc[:, t, :],
+                            lhsT=w1c[a, b][:, P * t : P * (t + 1)].bitcast(FP8X4),
+                            lhsT_scale=w1s[a, b][:, P * t : P * (t + 1)],
+                            rhs=vw[a, h][:, loc : loc + BANK_TOK].bitcast(FP8X4),
+                            rhs_scale=vs[a][:, j0 : j0 + BANK_TOK],
+                            start=(a == 0),
+                            stop=(a == 1),
+                        )
+                nc.scalar.activation(act[:, BANK_TOK * s : BANK_TOK * (s + 1), :], acc[:].rearrange("p t n -> p n t"), ACT.Silu)
+            hb = work.tile([P, CHUNK, PACK], BF16, name="hb", align_bytes=64)
+            nc.vector.tensor_tensor(hb[:], act[:], half_gain[:, b : b + 1, :].to_broadcast([P, CHUNK, PACK]), ALU.mult)
+            hc[b, u] = keep.tile([P, CHUNK], U32, name="hc%d%d" % (b, u), align_bytes=64)
+            hs[b, u] = keep.tile([P, CHUNK], U8, name="hs%d%d" % (b, u), align_bytes=64)
+            quantize(hc[b, u][:], hs[b, u][:], hb[:].rearrange("p n t -> p (n t)"))
+
+        out_v = out.rearrange("(c p) j -> p c j", p=P)
+
+        def final(u):
+            cols = slice(CHUNK * u, CHUNK * (u + 1))
+            for cc in range(2):
+                acc = psum_o.tile([P, 2, CHUNK], F32, name="acc_o")
+                for i in range(2):
+                    c = 2 * cc + i
+                    for b in range(2):
+                        nc.tensor.matmul_mx(
+                            out=acc[:, i, :],
+                            lhsT=w3c[b][:, P * c : P * (c + 1)].bitcast(FP8X4),
+                            lhsT_scale=w3s[b][:, P * c : P * (c + 1)],
+                            rhs=hc[b, u][:].bitcast(FP8X4),
+                            rhs_scale=hs[b, u][:],
+                            start=(b == 0),
+                            stop=(b == 1),
+                        )
+                res = work.tile([P, 2, CHUNK], F32, name="res")
+                nc.vector.scalar_tensor_tensor(res[:], th[:, 2 * cc : 2 * cc + 2, cols], 1.0, acc[:], ALU.add, ALU.mult)
+                nc.sync.dma_start(out_v[:, 2 * cc : 2 * cc + 2, cols], res[:])
+
+        gate(0)
+        load_w1(0, 0, "v", 1)
+        gate(1)
+        load_w1(1, 0, "v", 1)
+        load_w1(0, 1, "v", 1)
+        hidden(0, 0)
+        hidden(0, 1)
+        load_w1(1, 1, "s", 2)
+        hidden(0, 2)
+        hidden(0, 3)
+        hidden(1, 0)
+        load_w3(0, "s", 2)
+        hidden(1, 1)
+        load_w3(1, "s", 2)
+        final(0)
+        hidden(1, 2)
+        final(1)
+        hidden(1, 3)
+        final(2)
+        final(3)

@@ -22,6 +22,8 @@ KP = P * PACK
 HALF = 512
 CHUNK = 256
 BANK_TOK = 128
+SLOT_W4 = 8192
+SLOTS = (0, 10240, 18432)
 
 
 def tile_list_premise_slot_gate_kernel(tc, tab_words, tab_scales, offs, w1, w4_words, w4_scales, gain, w3, bg, out):
@@ -29,7 +31,7 @@ def tile_list_premise_slot_gate_kernel(tc, tab_words, tab_scales, offs, w1, w4_w
     with ExitStack() as ctx:
         keep = ctx.enter_context(tc.tile_pool(name="keep", bufs=1))
         stage = ctx.enter_context(tc.tile_pool(name="stage", bufs=1))
-        ring = ctx.enter_context(tc.tile_pool(name="ring", bufs=3))
+        ring = ctx.enter_context(tc.tile_pool(name="ring", bufs=1))
         work = ctx.enter_context(tc.tile_pool(name="work", bufs=3))
         psum_a = ctx.enter_context(tc.psum_pool(name="psum_a", bufs=4))
         psum_o = ctx.enter_context(tc.psum_pool(name="psum_o", bufs=4))
@@ -37,7 +39,7 @@ def tile_list_premise_slot_gate_kernel(tc, tab_words, tab_scales, offs, w1, w4_w
         offsets = keep.tile([P, S // 16], U16, name="offsets")
         nc.sync.dma_start(offsets[:], offs)
 
-        swin = ring.tile([P, T], U8, name="swin", tag="big", align_bytes=64)
+        swin = ring.tile([P, T], U8, name="swin", align_bytes=64, offset=SLOT_W4 - 1024)
         swin32 = swin[:].bitcast(I32)
         nc.gpsimd.memset(swin32, 0)
         ts32 = tab_scales.bitcast(I32)
@@ -48,18 +50,17 @@ def tile_list_premise_slot_gate_kernel(tc, tab_words, tab_scales, offs, w1, w4_w
         bg_sb = keep.tile([P, 4], F32, name="bg_sb")
         with nc.allow_non_contiguous_dma(reason="one bias value a partition"):
             nc.gpsimd.dma_start(bg_sb[:], bg.rearrange("(c p) -> p c", p=P))
-        gain_sb = keep.tile([P, 2, PACK], F32, name="gain_sb")
-        nc.sync.dma_start(gain_sb[:], gain.rearrange("(b p t) -> p b t", p=P, t=PACK))
+        gain_sb = keep.tile([P, 2, 8], F32, name="gain_sb")
+        for b in range(2):
+            nc.sync.dma_start(gain_sb[:, b, 0:PACK], gain[KP * b : KP * (b + 1)].rearrange("(p t) -> p t", t=PACK))
 
         tabs = []
 
         def load_tab(a):
-            tab = ring.tile([P, T], U32, name="tab%d" % a, tag="big", align_bytes=64)
+            tab = ring.tile([P, T], U32, name="tab%d" % a, align_bytes=64, offset=SLOTS[1 + a])
             nc.sync.dma_start(tab[:].bitcast(I32), tab_words[a].rearrange("p t i -> p (t i)").bitcast(I32))
             tabs.append(tab)
 
-        w4c = keep.tile([P, 2, 2 * N], U8, name="w4c", align_bytes=64)
-        nc.sync.dma_start(w4c[:].bitcast(I32), w4_words.bitcast(I32).rearrange("a p n -> p a n"))
         load_tab(0)
         w4s = keep.tile([P, 2, N], U8, name="w4s", align_bytes=64)
         nc.vector.memset(w4s[:].bitcast(I32), 0)
@@ -93,7 +94,7 @@ def tile_list_premise_slot_gate_kernel(tc, tab_words, tab_scales, offs, w1, w4_w
         half_bg = keep.tile([P, 4], F32, name="half_bg")
         nc.gpsimd.tensor_scalar(half_bg[:], bg_sb[:], 0.5, 0.0, ALU.mult, ALU.add)
         half_gain = keep.tile([P, 2, PACK], F32, name="half_gain")
-        nc.gpsimd.tensor_scalar(half_gain[:], gain_sb[:], 0.5, 0.0, ALU.mult, ALU.add)
+        nc.gpsimd.tensor_scalar(half_gain[:], gain_sb[:, :, 0:PACK], 0.5, 0.0, ALU.mult, ALU.add)
 
         def quantize(codes, scales, src):
             nc.vector.quantize_mx(out=codes.bitcast(FP8X4), scales=scales, in_=src)
@@ -106,16 +107,15 @@ def tile_list_premise_slot_gate_kernel(tc, tab_words, tab_scales, offs, w1, w4_w
 
         w1c, w1s = {}, {}
 
-        def load_w1(a, b, engine, pieces):
-            raw = ring.tile([P, PACK, KP], F32, name="raw1", tag="big", align_bytes=64)
+        def load_w1(a, b, shares):
+            raw = ring.tile([P, PACK, KP], F32, name="raw1_%d%d" % (a, b), align_bytes=64, offset=SLOTS[(2 * b + a) % 3])
             nc.sync.dma_start(raw[:], w1[KP * a : KP * (a + 1), KP * b : KP * (b + 1)].rearrange("(p j) c -> p j c", j=PACK))
             grp = stage.tile([P, PACK, P, PACK], BF16, name="grp", align_bytes=64)
-            step = P // pieces
-            for m0 in range(0, P, step):
+            for engine, m0, m1 in shares:
                 copy_on(
                     engine,
-                    grp[:, :, m0 : m0 + step, :].rearrange("p t m j -> p m j t"),
-                    raw[:].rearrange("p j (m t) -> p m j t", t=PACK)[:, m0 : m0 + step],
+                    grp[:, :, m0:m1, :].rearrange("p t m j -> p m j t"),
+                    raw[:].rearrange("p j (m t) -> p m j t", t=PACK)[:, m0:m1],
                 )
             w1c[a, b] = keep.tile([P, KP], U32, name="w1c%d%d" % (a, b), align_bytes=64)
             w1s[a, b] = keep.tile([P, KP], U8, name="w1s%d%d" % (a, b), align_bytes=64)
@@ -123,16 +123,29 @@ def tile_list_premise_slot_gate_kernel(tc, tab_words, tab_scales, offs, w1, w4_w
 
         w3c, w3s = {}, {}
 
-        def load_w3(b, engine, pieces):
-            raw = ring.tile([P, PACK, N], F32, name="raw3", tag="big", align_bytes=64)
+        def load_w1_halves(a, b):
+            grp = stage.tile([P, PACK, P, PACK], BF16, name="grp", align_bytes=64)
+            for i in range(2):
+                raw = ring.tile([P, PACK, KP // 2], F32, name="rawh_%d" % i, align_bytes=64, offset=SLOTS[(2 * b + a) % 3] + 4096 * i)
+                c0 = KP * b + (KP // 2) * i
+                nc.sync.dma_start(raw[:], w1[KP * a : KP * (a + 1), c0 : c0 + KP // 2].rearrange("(p j) c -> p j c", j=PACK))
+                nc.vector.tensor_copy(
+                    grp[:, :, 64 * i : 64 * (i + 1), :].rearrange("p t m j -> p m j t"),
+                    raw[:].rearrange("p j (m t) -> p m j t", t=PACK),
+                )
+            w1c[a, b] = keep.tile([P, KP], U32, name="w1c%d%d" % (a, b), align_bytes=64)
+            w1s[a, b] = keep.tile([P, KP], U8, name="w1s%d%d" % (a, b), align_bytes=64)
+            quantize(w1c[a, b][:], w1s[a, b][:], grp[:].rearrange("p t m j -> p (t m j)"))
+
+        def load_w3(b, shares):
+            raw = ring.tile([P, PACK, N], F32, name="raw3_%d" % b, align_bytes=64, offset=SLOTS[1 + b])
             nc.sync.dma_start(raw[:], w3[KP * b : KP * (b + 1), :].rearrange("(p j) n -> p j n", j=PACK))
             grp = stage.tile([P, N, PACK], BF16, name="grp", align_bytes=64)
-            step = (N // 4) // pieces
-            for c0 in range(0, N // 4, step):
+            for engine, c0, c1 in shares:
                 copy_on(
                     engine,
-                    grp[:].rearrange("p (c i) j -> p c j i", i=4)[:, c0 : c0 + step],
-                    raw[:].rearrange("p j (c i) -> p c j i", i=4)[:, c0 : c0 + step],
+                    grp[:].rearrange("p (c i) j -> p c j i", i=4)[:, c0:c1],
+                    raw[:].rearrange("p j (c i) -> p c j i", i=4)[:, c0:c1],
                 )
             w3c[b] = keep.tile([P, N], U32, name="w3c%d" % b, align_bytes=64)
             w3s[b] = keep.tile([P, N], U8, name="w3s%d" % b, align_bytes=64)
@@ -182,6 +195,36 @@ def tile_list_premise_slot_gate_kernel(tc, tab_words, tab_scales, offs, w1, w4_w
             hs[b, u] = keep.tile([P, CHUNK], U8, name="hs%d%d" % (b, u), align_bytes=64)
             quantize(hc[b, u][:], hs[b, u][:], hb[:].rearrange("p n t -> p (n t)"))
 
+        def hidden_gain_on_scalar(b, u):
+            act = work.tile([P, PACK, CHUNK], F32, name="act")
+            j0 = CHUNK * u
+            h, loc = divmod(j0, HALF)
+            for s in range(2):
+                acc = psum_a.tile([P, 2, CHUNK], F32, name="acc_a")
+                for i in range(2):
+                    t = 2 * s + i
+                    for a in range(2):
+                        nc.tensor.matmul_mx(
+                            out=acc[:, i, :],
+                            lhsT=w1c[a, b][:, P * t : P * (t + 1)].bitcast(FP8X4),
+                            lhsT_scale=w1s[a, b][:, P * t : P * (t + 1)],
+                            rhs=vw[a, h][:, loc : loc + CHUNK].bitcast(FP8X4),
+                            rhs_scale=vs[a][:, j0 : j0 + CHUNK],
+                            start=(a == 0),
+                            stop=(a == 1),
+                        )
+                nc.scalar.activation(act[:, 2 * s : 2 * s + 2, :], acc[:], ACT.Silu)
+            rows = work.tile([P, PACK, CHUNK], BF16, name="rows", align_bytes=64)
+            for t in range(PACK):
+                nc.scalar.activation(rows[:, t, :], act[:, t, :], ACT.Copy, scale=half_gain[:, b, t : t + 1])
+            hb = work.tile([P, CHUNK, PACK], BF16, name="hb", align_bytes=64)
+            nc.vector.tensor_copy(
+                hb[:].rearrange("p (c i) t -> p c t i", i=4), rows[:].rearrange("p t (c i) -> p c t i", i=4)
+            )
+            hc[b, u] = keep.tile([P, CHUNK], U32, name="hc%d%d" % (b, u), align_bytes=64)
+            hs[b, u] = keep.tile([P, CHUNK], U8, name="hs%d%d" % (b, u), align_bytes=64)
+            quantize(hc[b, u][:], hs[b, u][:], hb[:].rearrange("p n t -> p (n t)"))
+
         out_v = out.rearrange("(c p) j -> p c j", p=P)
 
         def final(u):
@@ -200,26 +243,30 @@ def tile_list_premise_slot_gate_kernel(tc, tab_words, tab_scales, offs, w1, w4_w
                             start=(b == 0),
                             stop=(b == 1),
                         )
-                res = work.tile([P, 2, CHUNK], F32, name="res")
+                res = work.tile([P, 2, CHUNK], F32, name="res", bufs=8)
                 nc.vector.scalar_tensor_tensor(res[:], th[:, 2 * cc : 2 * cc + 2, cols], 1.0, acc[:], ALU.add, ALU.mult)
                 nc.sync.dma_start(out_v[:, 2 * cc : 2 * cc + 2, cols], res[:])
 
+        on_v = [("v", 0, P)]
+        on_s = [("s", 0, 64), ("s", 64, P)]
+        load_w1(0, 0, on_v)
+        w4c = ring.tile([P, 2, 2 * N], U8, name="w4c", align_bytes=64, offset=SLOT_W4)
+        nc.sync.dma_start(w4c[:].bitcast(I32), w4_words.bitcast(I32).rearrange("a p n -> p a n"))
         gate(0)
-        load_w1(0, 0, "v", 1)
+        load_w1_halves(1, 0)
         gate(1)
-        load_w1(1, 0, "v", 1)
-        load_w1(0, 1, "v", 1)
+        load_w1(0, 1, on_v)
         hidden(0, 0)
         hidden(0, 1)
-        load_w1(1, 1, "s", 2)
+        load_w1(1, 1, on_s)
         hidden(0, 2)
         hidden(0, 3)
         hidden(1, 0)
-        load_w3(0, "s", 2)
-        hidden(1, 1)
-        load_w3(1, "s", 2)
+        load_w3(0, on_s)
+        load_w3(1, on_v)
+        hidden_gain_on_scalar(1, 1)
         final(0)
-        hidden(1, 2)
+        hidden_gain_on_scalar(1, 2)
         final(1)
         hidden(1, 3)
         final(2)

@@ -22,15 +22,14 @@ KP = P * PACK
 HALF = 512
 CHUNK = 256
 BANK_TOK = 128
-SLOT_W4 = 8192
-SLOTS = (0, 10240, 18432)
+SLOTS = (0, 8192, 16384)
 
 
 def tile_list_premise_slot_gate_kernel(tc, tab_words, tab_scales, offs, w1, w4_words, w4_scales, gain, w3, bg, out):
     nc = tc.nc
     with ExitStack() as ctx:
         keep = ctx.enter_context(tc.tile_pool(name="keep", bufs=1))
-        stage = ctx.enter_context(tc.tile_pool(name="stage", bufs=1))
+        stage = ctx.enter_context(tc.tile_pool(name="stage", bufs=3))
         ring = ctx.enter_context(tc.tile_pool(name="ring", bufs=1))
         work = ctx.enter_context(tc.tile_pool(name="work", bufs=3))
         psum_a = ctx.enter_context(tc.psum_pool(name="psum_a", bufs=4))
@@ -39,7 +38,7 @@ def tile_list_premise_slot_gate_kernel(tc, tab_words, tab_scales, offs, w1, w4_w
         offsets = keep.tile([P, S // 16], U16, name="offsets")
         nc.sync.dma_start(offsets[:], offs)
 
-        swin = ring.tile([P, T], U8, name="swin", align_bytes=64, offset=SLOT_W4 - 1024)
+        swin = ring.tile([P, T], U8, name="swin", align_bytes=64, offset=SLOTS[0])
         swin32 = swin[:].bitcast(I32)
         nc.gpsimd.memset(swin32, 0)
         ts32 = tab_scales.bitcast(I32)
@@ -50,9 +49,10 @@ def tile_list_premise_slot_gate_kernel(tc, tab_words, tab_scales, offs, w1, w4_w
         bg_sb = keep.tile([P, 4], F32, name="bg_sb")
         with nc.allow_non_contiguous_dma(reason="one bias value a partition"):
             nc.gpsimd.dma_start(bg_sb[:], bg.rearrange("(c p) -> p c", p=P))
-        gain_sb = keep.tile([P, 2, 8], F32, name="gain_sb")
-        for b in range(2):
-            nc.sync.dma_start(gain_sb[:, b, 0:PACK], gain[KP * b : KP * (b + 1)].rearrange("(p t) -> p t", t=PACK))
+        gain_sb = keep.tile([P, 2, PACK], F32, name="gain_sb")
+        nc.sync.dma_start(gain_sb[:], gain.rearrange("(b p t) -> p b t", p=P, t=PACK))
+        w4c = keep.tile([P, 2, 2 * N], U8, name="w4c", align_bytes=64)
+        nc.sync.dma_start(w4c[:].bitcast(I32), w4_words.bitcast(I32).rearrange("a p n -> p a n"))
 
         tabs = []
 
@@ -94,7 +94,7 @@ def tile_list_premise_slot_gate_kernel(tc, tab_words, tab_scales, offs, w1, w4_w
         half_bg = keep.tile([P, 4], F32, name="half_bg")
         nc.gpsimd.tensor_scalar(half_bg[:], bg_sb[:], 0.5, 0.0, ALU.mult, ALU.add)
         half_gain = keep.tile([P, 2, PACK], F32, name="half_gain")
-        nc.gpsimd.tensor_scalar(half_gain[:], gain_sb[:, :, 0:PACK], 0.5, 0.0, ALU.mult, ALU.add)
+        nc.gpsimd.tensor_scalar(half_gain[:], gain_sb[:], 0.5, 0.0, ALU.mult, ALU.add)
 
         def quantize(codes, scales, src):
             nc.vector.quantize_mx(out=codes.bitcast(FP8X4), scales=scales, in_=src)
@@ -248,26 +248,24 @@ def tile_list_premise_slot_gate_kernel(tc, tab_words, tab_scales, offs, w1, w4_w
                 nc.sync.dma_start(out_v[:, 2 * cc : 2 * cc + 2, cols], res[:])
 
         on_v = [("v", 0, P)]
-        on_s = [("s", 0, 64), ("s", 64, P)]
-        load_w1(0, 0, on_v)
-        w4c = ring.tile([P, 2, 2 * N], U8, name="w4c", align_bytes=64, offset=SLOT_W4)
-        nc.sync.dma_start(w4c[:].bitcast(I32), w4_words.bitcast(I32).rearrange("a p n -> p a n"))
+        on_s = [("s", 0, P)]
         gate(0)
-        load_w1_halves(1, 0)
+        load_w1(0, 0, on_v)
         gate(1)
+        load_w1_halves(1, 0)
         load_w1(0, 1, on_v)
         hidden(0, 0)
         hidden(0, 1)
-        load_w1(1, 1, on_s)
+        load_w1(1, 1, on_v)
         hidden(0, 2)
         hidden(0, 3)
-        hidden(1, 0)
         load_w3(0, on_s)
-        load_w3(1, on_v)
-        hidden_gain_on_scalar(1, 1)
+        hidden(1, 0)
+        load_w3(1, on_s)
+        hidden(1, 1)
         final(0)
         hidden_gain_on_scalar(1, 2)
         final(1)
-        hidden(1, 3)
+        hidden_gain_on_scalar(1, 3)
         final(2)
         final(3)

@@ -252,11 +252,11 @@ def tile_list_premise_slot_gate_kernel(tc, tab_words, tab_scales, offs, w1, w4_w
         gate(0)
         load_w1(0, 0, on_v)
         gate(1)
-        load_w1_halves(1, 0)
+        load_w1(1, 0, on_v)
         load_w1(0, 1, on_v)
+        load_w1(1, 1, on_v)
         hidden(0, 0)
         hidden(0, 1)
-        load_w1(1, 1, on_v)
         hidden(0, 2)
         hidden(0, 3)
         load_w3(0, on_s)

@@ -40,17 +40,19 @@ def tile_list_premise_slot_gate_kernel(tc, tab_words, tab_scales, offs, w1, w4_w
 
         swin = ring.tile([P, T], U8, name="swin", align_bytes=64, offset=SLOTS[0])
         swin32 = swin[:].bitcast(I32)
-        nc.gpsimd.memset(swin32, 0)
+        nc.vector.memset(swin32, 0)
         ts32 = tab_scales.bitcast(I32)
         for a in range(2):
             for e in range(2):
                 nc.sync.dma_start(swin32[2 * a + e : P : 16, :], ts32[a, e:16:2, :])
 
+        w4s = keep.tile([P, 2, N], U8, name="w4s", align_bytes=64)
+        nc.gpsimd.memset(w4s[:].bitcast(I32), 0)
         bg_sb = keep.tile([P, 4], F32, name="bg_sb")
         with nc.allow_non_contiguous_dma(reason="one bias value a partition"):
             nc.gpsimd.dma_start(bg_sb[:], bg.rearrange("(c p) -> p c", p=P))
         gain_sb = keep.tile([P, 2, PACK], F32, name="gain_sb")
-        nc.sync.dma_start(gain_sb[:], gain.rearrange("(b p t) -> p b t", p=P, t=PACK))
+        nc.gpsimd.dma_start(gain_sb[:], gain.rearrange("(b p t) -> p b t", p=P, t=PACK))
         w4c = keep.tile([P, 2, 2 * N], U8, name="w4c", align_bytes=64)
         nc.sync.dma_start(w4c[:].bitcast(I32), w4_words.bitcast(I32).rearrange("a p n -> p a n"))
 
@@ -62,8 +64,6 @@ def tile_list_premise_slot_gate_kernel(tc, tab_words, tab_scales, offs, w1, w4_w
             tabs.append(tab)
 
         load_tab(0)
-        w4s = keep.tile([P, 2, N], U8, name="w4s", align_bytes=64)
-        nc.vector.memset(w4s[:].bitcast(I32), 0)
         w4s_src = w4_scales.bitcast(I32).rearrange("a q n -> q a n")
         for d in range(4):
             nc.sync.dma_start(w4s[:].bitcast(I32)[32 * d : 32 * d + 4], w4s_src[4 * d : 4 * d + 4])
@@ -92,9 +92,9 @@ def tile_list_premise_slot_gate_kernel(tc, tab_words, tab_scales, offs, w1, w4_w
                 vw[a, h] = g
 
         half_bg = keep.tile([P, 4], F32, name="half_bg")
-        nc.gpsimd.tensor_scalar(half_bg[:], bg_sb[:], 0.5, 0.0, ALU.mult, ALU.add)
+        nc.scalar.activation(half_bg[:], bg_sb[:], ACT.Copy, scale=0.5)
         half_gain = keep.tile([P, 2, PACK], F32, name="half_gain")
-        nc.gpsimd.tensor_scalar(half_gain[:], gain_sb[:], 0.5, 0.0, ALU.mult, ALU.add)
+        nc.scalar.activation(half_gain[:], gain_sb[:], ACT.Copy, scale=0.5)
 
         def quantize(codes, scales, src):
             nc.vector.quantize_mx(out=codes.bitcast(FP8X4), scales=scales, in_=src)
@@ -107,21 +107,10 @@ def tile_list_premise_slot_gate_kernel(tc, tab_words, tab_scales, offs, w1, w4_w
 
         w1c, w1s = {}, {}
 
-        def load_w1(a, b, shares):
+        def cast_w1(a, b, grp):
             raw = ring.tile([P, PACK, KP], F32, name="raw1_%d%d" % (a, b), align_bytes=64, offset=SLOTS[(2 * b + a) % 3])
             nc.sync.dma_start(raw[:], w1[KP * a : KP * (a + 1), KP * b : KP * (b + 1)].rearrange("(p j) c -> p j c", j=PACK))
-            grp = stage.tile([P, PACK, P, PACK], BF16, name="grp", align_bytes=64)
-            for engine, m0, m1 in shares:
-                copy_on(
-                    engine,
-                    grp[:, :, m0:m1, :].rearrange("p t m j -> p m j t"),
-                    raw[:].rearrange("p j (m t) -> p m j t", t=PACK)[:, m0:m1],
-                )
-            w1c[a, b] = keep.tile([P, KP], U32, name="w1c%d%d" % (a, b), align_bytes=64)
-            w1s[a, b] = keep.tile([P, KP], U8, name="w1s%d%d" % (a, b), align_bytes=64)
-            quantize(w1c[a, b][:], w1s[a, b][:], grp[:].rearrange("p t m j -> p (t m j)"))
-
-        w3c, w3s = {}, {}
+            nc.vector.tensor_copy(grp.rearrange("p t m j -> p m j t"), raw[:].rearrange("p j (m t) -> p m j t", t=PACK))
 
         def load_w1_halves(a, b):
             grp = stage.tile([P, PACK, P, PACK], BF16, name="grp", align_bytes=64)
@@ -133,9 +122,34 @@ def tile_list_premise_slot_gate_kernel(tc, tab_words, tab_scales, offs, w1, w4_w
                     grp[:, :, 64 * i : 64 * (i + 1), :].rearrange("p t m j -> p m j t"),
                     raw[:].rearrange("p j (m t) -> p m j t", t=PACK),
                 )
-            w1c[a, b] = keep.tile([P, KP], U32, name="w1c%d%d" % (a, b), align_bytes=64)
-            w1s[a, b] = keep.tile([P, KP], U8, name="w1s%d%d" % (a, b), align_bytes=64)
-            quantize(w1c[a, b][:], w1s[a, b][:], grp[:].rearrange("p t m j -> p (t m j)"))
+            codes = keep.tile([P, KP], U32, name="w1c%d%d" % (a, b), align_bytes=64)
+            scales = keep.tile([P, KP], U8, name="w1s%d%d" % (a, b), align_bytes=64)
+            quantize(codes[:], scales[:], grp[:].rearrange("p t m j -> p (t m j)"))
+            w1c[a, b], w1s[a, b] = codes[:], scales[:]
+
+        def load_w1(a, b):
+            if a != b:
+                grp = keep.tile([P, PACK, P, PACK], BF16, name="grp_mid", align_bytes=64)
+            else:
+                grp = stage.tile([P, PACK, P, PACK], BF16, name="grp", align_bytes=64)
+            cast_w1(a, b, grp[:])
+            codes = keep.tile([P, KP], U32, name="w1c%d%d" % (a, b), align_bytes=64)
+            scales = keep.tile([P, KP], U8, name="w1s%d%d" % (a, b), align_bytes=64)
+            quantize(codes[:], scales[:], grp[:].rearrange("p t m j -> p (t m j)"))
+            w1c[a, b], w1s[a, b] = codes[:], scales[:]
+
+        def quantize_w1_pair(b, grp2):
+            codes = keep.tile([P, 2, KP], U32, name="w1c%d" % b, align_bytes=64)
+            scales = keep.tile([P, 2, KP], U8, name="w1s%d" % b, align_bytes=64)
+            quantize(
+                codes[:].rearrange("p a c -> p (a c)"),
+                scales[:].rearrange("p a c -> p (a c)"),
+                grp2[:].rearrange("p a t m j -> p (a t m j)"),
+            )
+            for a in range(2):
+                w1c[a, b], w1s[a, b] = codes[:, a, :], scales[:, a, :]
+
+        w3c, w3s = {}, {}
 
         def load_w3(b, shares):
             raw = ring.tile([P, PACK, N], F32, name="raw3_%d" % b, align_bytes=64, offset=SLOTS[1 + b])
@@ -169,103 +183,128 @@ def tile_list_premise_slot_gate_kernel(tc, tab_words, tab_scales, offs, w1, w4_w
                     )
                 nc.scalar.activation(th[:, c, cols], acc[:], ACT.Tanh, bias=half_bg[:, c : c + 1], scale=0.5)
 
-        hc, hs = {}, {}
+        hc = [keep.tile([P, S], U32, name="hc%d" % b, align_bytes=64) for b in range(2)]
+        hs = [keep.tile([P, S], U8, name="hs%d" % b, align_bytes=64) for b in range(2)]
 
-        def hidden(b, u):
-            act = work.tile([P, CHUNK, PACK], F32, name="act")
-            for s in range(CHUNK // BANK_TOK):
-                j0 = CHUNK * u + BANK_TOK * s
-                h, loc = divmod(j0, HALF)
-                acc = psum_a.tile([P, PACK, BANK_TOK], F32, name="acc_a")
-                for t in range(PACK):
-                    for a in range(2):
-                        nc.tensor.matmul_mx(
-                            out=acc[:, t, :],
-                            lhsT=w1c[a, b][:, P * t : P * (t + 1)].bitcast(FP8X4),
-                            lhsT_scale=w1s[a, b][:, P * t : P * (t + 1)],
-                            rhs=vw[a, h][:, loc : loc + BANK_TOK].bitcast(FP8X4),
-                            rhs_scale=vs[a][:, j0 : j0 + BANK_TOK],
-                            start=(a == 0),
-                            stop=(a == 1),
-                        )
-                nc.scalar.activation(act[:, BANK_TOK * s : BANK_TOK * (s + 1), :], acc[:].rearrange("p t n -> p n t"), ACT.Silu)
-            hb = work.tile([P, CHUNK, PACK], BF16, name="hb", align_bytes=64)
-            nc.vector.tensor_tensor(hb[:], act[:], half_gain[:, b : b + 1, :].to_broadcast([P, CHUNK, PACK]), ALU.mult)
-            hc[b, u] = keep.tile([P, CHUNK], U32, name="hc%d%d" % (b, u), align_bytes=64)
-            hs[b, u] = keep.tile([P, CHUNK], U8, name="hs%d%d" % (b, u), align_bytes=64)
-            quantize(hc[b, u][:], hs[b, u][:], hb[:].rearrange("p n t -> p (n t)"))
-
-        def hidden_gain_on_scalar(b, u):
-            act = work.tile([P, PACK, CHUNK], F32, name="act")
-            j0 = CHUNK * u
+        def first_product(acc, b, t0, j0, n):
             h, loc = divmod(j0, HALF)
+            slices = acc.shape[1]
+            passes = [(a, i) for a in range(2) for i in range(slices)]
+            if b == 1:
+                passes = [(a, i) for i in range(slices) for a in range(2)]
+            for a, i in passes:
+                t = t0 + i
+                nc.tensor.matmul_mx(
+                    out=acc[:, i, :],
+                    lhsT=w1c[a, b][:, P * t : P * (t + 1)].bitcast(FP8X4),
+                    lhsT_scale=w1s[a, b][:, P * t : P * (t + 1)],
+                    rhs=vw[a, h][:, loc : loc + n].bitcast(FP8X4),
+                    rhs_scale=vs[a][:, j0 : j0 + n],
+                    start=((a, i) == passes[0]),
+                    stop=((a, i) == passes[-1]),
+                )
+
+        def gain_v(b, j0, n, hb):
+            act = work.tile([P, 2, n, 2], F32, name="act", bufs=5)
             for s in range(2):
-                acc = psum_a.tile([P, 2, CHUNK], F32, name="acc_a")
-                for i in range(2):
-                    t = 2 * s + i
-                    for a in range(2):
-                        nc.tensor.matmul_mx(
-                            out=acc[:, i, :],
-                            lhsT=w1c[a, b][:, P * t : P * (t + 1)].bitcast(FP8X4),
-                            lhsT_scale=w1s[a, b][:, P * t : P * (t + 1)],
-                            rhs=vw[a, h][:, loc : loc + CHUNK].bitcast(FP8X4),
-                            rhs_scale=vs[a][:, j0 : j0 + CHUNK],
-                            start=(a == 0),
-                            stop=(a == 1),
-                        )
-                nc.scalar.activation(act[:, 2 * s : 2 * s + 2, :], acc[:], ACT.Silu)
-            rows = work.tile([P, PACK, CHUNK], BF16, name="rows", align_bytes=64)
+                acc = psum_a.tile([P, 2, n], F32, name="acc_a")
+                first_product(acc, b, 2 * s, j0, n)
+                nc.scalar.activation(act[:, s], acc[:].rearrange("p e n -> p n e"), ACT.Silu)
+            nc.vector.tensor_tensor(
+                hb.rearrange("p n (s e) -> p n s e", e=2),
+                act[:].rearrange("p s n e -> p n s e"),
+                half_gain[:, b : b + 1, :].rearrange("p o (s e) -> p o s e", e=2).to_broadcast([P, n, 2, 2]),
+                ALU.mult,
+            )
+
+        def quantize_h(b, j0, n, hb):
+            quantize(hc[b][:, j0 : j0 + n], hs[b][:, j0 : j0 + n], hb.rearrange("p n t -> p (n t)"))
+
+        def hidden_v(b, j0, n):
+            if b == 0:
+                hb = ring.tile([P, n, PACK], BF16, name="hb0_%d" % j0, align_bytes=64, offset=SLOTS[0] + 2 * PACK * j0)
+            else:
+                hb = work.tile([P, n, PACK], BF16, name="hb", align_bytes=64)
+            gain_v(b, j0, n, hb[:])
+            quantize_h(b, j0, n, hb[:])
+
+        def hidden_s(b, j0, n, shares):
+            act = work.tile([P, PACK, n], F32, name="act", bufs=5)
+            per_bank = HALF // n
+            for s in range(PACK // per_bank):
+                acc = psum_a.tile([P, per_bank, n], F32, name="acc_a")
+                first_product(acc, b, per_bank * s, j0, n)
+                nc.scalar.activation(act[:, per_bank * s : per_bank * (s + 1), :], acc[:], ACT.Silu)
+            rows = work.tile([P, PACK, n], BF16, name="rows", align_bytes=64)
             for t in range(PACK):
                 nc.scalar.activation(rows[:, t, :], act[:, t, :], ACT.Copy, scale=half_gain[:, b, t : t + 1])
-            hb = work.tile([P, CHUNK, PACK], BF16, name="hb", align_bytes=64)
-            nc.vector.tensor_copy(
-                hb[:].rearrange("p (c i) t -> p c t i", i=4), rows[:].rearrange("p t (c i) -> p c t i", i=4)
-            )
-            hc[b, u] = keep.tile([P, CHUNK], U32, name="hc%d%d" % (b, u), align_bytes=64)
-            hs[b, u] = keep.tile([P, CHUNK], U8, name="hs%d%d" % (b, u), align_bytes=64)
-            quantize(hc[b, u][:], hs[b, u][:], hb[:].rearrange("p n t -> p (n t)"))
+            hb = work.tile([P, n, PACK], BF16, name="hb", align_bytes=64)
+            for engine, c0, c1 in shares:
+                copy_on(
+                    engine,
+                    hb[:].rearrange("p (c i) t -> p c t i", i=8)[:, c0:c1],
+                    rows[:].rearrange("p t (c i) -> p c t i", i=8)[:, c0:c1],
+                )
+            quantize(hc[b][:, j0 : j0 + n], hs[b][:, j0 : j0 + n], hb[:].rearrange("p n t -> p (n t)"))
 
         out_v = out.rearrange("(c p) j -> p c j", p=P)
 
-        def final(u):
-            cols = slice(CHUNK * u, CHUNK * (u + 1))
-            for cc in range(2):
-                acc = psum_o.tile([P, 2, CHUNK], F32, name="acc_o")
-                for i in range(2):
-                    c = 2 * cc + i
-                    for b in range(2):
-                        nc.tensor.matmul_mx(
-                            out=acc[:, i, :],
-                            lhsT=w3c[b][:, P * c : P * (c + 1)].bitcast(FP8X4),
-                            lhsT_scale=w3s[b][:, P * c : P * (c + 1)],
-                            rhs=hc[b, u][:].bitcast(FP8X4),
-                            rhs_scale=hs[b, u][:],
-                            start=(b == 0),
-                            stop=(b == 1),
-                        )
-                res = work.tile([P, 2, CHUNK], F32, name="res", bufs=8)
-                nc.vector.scalar_tensor_tensor(res[:], th[:, 2 * cc : 2 * cc + 2, cols], 1.0, acc[:], ALU.add, ALU.mult)
-                nc.sync.dma_start(out_v[:, 2 * cc : 2 * cc + 2, cols], res[:])
+        def final(j0, n, last=False):
+            cols = slice(j0, j0 + n)
+            per_bank = HALF // n
+            for cc in range(4 // per_bank):
+                acc = psum_o.tile([P, per_bank, n], F32, name="acc_o")
+                passes = [(b, i) for i in range(per_bank) for b in range(2)]
+                if last:
+                    passes = [(b, i) for b in range(2) for i in range(per_bank)]
+                for b, i in passes:
+                    c = per_bank * cc + i
+                    nc.tensor.matmul_mx(
+                        out=acc[:, i, :],
+                        lhsT=w3c[b][:, P * c : P * (c + 1)].bitcast(FP8X4),
+                        lhsT_scale=w3s[b][:, P * c : P * (c + 1)],
+                        rhs=hc[b][:, cols].bitcast(FP8X4),
+                        rhs_scale=hs[b][:, cols],
+                        start=((b, i) == passes[0]),
+                        stop=((b, i) == passes[-1]),
+                    )
+                step = 1 if last and cc == 4 // per_bank - 1 else per_bank
+                for i in range(0, per_bank, step):
+                    c0 = per_bank * cc + i
+                    res = work.tile([P, step, n], F32, name="res", bufs=9)
+                    nc.vector.scalar_tensor_tensor(res[:], th[:, c0 : c0 + step, cols], 1.0, acc[:, i : i + step, :], ALU.add, ALU.mult)
+                    nc.sync.dma_start(out_v[:, c0 : c0 + step, cols], res[:])
 
         on_v = [("v", 0, P)]
         on_s = [("s", 0, P)]
+        idle = psum_a.tile([P, HALF], F32, name="acc_a")
+        for c in range(3):
+            nc.tensor.matmul_mx(
+                out=idle[:],
+                lhsT=w4c[:, 0, 2 * P * c : 2 * P * (c + 1)].bitcast(FP4X4),
+                lhsT_scale=w4s[:, 0, P * c : P * (c + 1)],
+                rhs=vw[0, 0][:].bitcast(FP8X4),
+                rhs_scale=sg[:, 0:HALF],
+                start=True,
+                stop=True,
+            )
         gate(0)
-        load_w1(0, 0, on_v)
+        load_w1(0, 0)
         gate(1)
-        load_w1(1, 0, on_v)
-        load_w1(0, 1, on_v)
-        load_w1(1, 1, on_v)
-        hidden(0, 0)
-        hidden(0, 1)
-        hidden(0, 2)
-        hidden(0, 3)
+        load_w1(1, 0)
+        load_w1(0, 1)
+        load_w1_halves(1, 1)
+        hidden_v(0, 0, 256)
+        hidden_v(0, 256, 256)
+        hidden_v(0, 512, 256)
+        hidden_v(0, 768, 256)
         load_w3(0, on_s)
-        hidden(1, 0)
+        hidden_v(1, 0, 256)
         load_w3(1, on_s)
-        hidden(1, 1)
-        final(0)
-        hidden_gain_on_scalar(1, 2)
-        final(1)
-        hidden_gain_on_scalar(1, 3)
-        final(2)
-        final(3)
+        hidden_v(1, 256, 256)
+        final(0, 256)
+        hidden_s(1, 512, 256, [("v", 0, 32)])
+        final(256, 256)
+        hidden_s(1, 768, 256, [("s", 0, 16), ("v", 16, 32)])
+        final(512, 256)
+        final(768, 256, last=True)

@@ -1,6 +1,7 @@
 from contextlib import ExitStack
 
 import concourse.mybir as mybir
+from concourse.masks import make_identity
 
 K, T, S, H, N = 1024, 2048, 1024, 1024, 512
 FLOPS = 2 * S * (K * H + K * N + H * N)
@@ -23,17 +24,21 @@ HALF = 512
 CHUNK = 256
 BANK_TOK = 128
 SLOTS = (0, 8192, 16384)
+TH_AT = 24576
+GRP_AT = TH_AT + 16384
+G_CUTS = (0, 176, 352, 512)
 
 
 def tile_list_premise_slot_gate_kernel(tc, tab_words, tab_scales, offs, w1, w4_words, w4_scales, gain, w3, bg, out):
     nc = tc.nc
     with ExitStack() as ctx:
         keep = ctx.enter_context(tc.tile_pool(name="keep", bufs=1))
-        stage = ctx.enter_context(tc.tile_pool(name="stage", bufs=3))
         ring = ctx.enter_context(tc.tile_pool(name="ring", bufs=1))
         work = ctx.enter_context(tc.tile_pool(name="work", bufs=3))
-        psum_a = ctx.enter_context(tc.psum_pool(name="psum_a", bufs=4))
-        psum_o = ctx.enter_context(tc.psum_pool(name="psum_o", bufs=4))
+        psum = ctx.enter_context(tc.psum_pool(name="psum", bufs=1))
+
+        def bank(i, shape, name):
+            return psum.tile(shape, F32, name=name, offset=2048 * i)
 
         offsets = keep.tile([P, S // 16], U16, name="offsets")
         nc.sync.dma_start(offsets[:], offs)
@@ -48,11 +53,12 @@ def tile_list_premise_slot_gate_kernel(tc, tab_words, tab_scales, offs, w1, w4_w
 
         w4s = keep.tile([P, 2, N], U8, name="w4s", align_bytes=64)
         nc.gpsimd.memset(w4s[:].bitcast(I32), 0)
-        bg_sb = keep.tile([P, 4], F32, name="bg_sb")
-        with nc.allow_non_contiguous_dma(reason="one bias value a partition"):
-            nc.gpsimd.dma_start(bg_sb[:], bg.rearrange("(c p) -> p c", p=P))
-        gain_sb = keep.tile([P, 2, PACK], F32, name="gain_sb")
-        nc.gpsimd.dma_start(gain_sb[:], gain.rearrange("(b p t) -> p b t", p=P, t=PACK))
+        gain_rows_in = keep.tile([P, KP], F32, name="gain_rows_in")
+        nc.gpsimd.memset(gain_rows_in[:], 0.0)
+        nc.scalar.dma_start(gain_rows_in[0:2, :], gain.rearrange("(b r) -> b r", b=2))
+        bias_rows_in = keep.tile([P, P], F32, name="bias_rows_in")
+        nc.gpsimd.memset(bias_rows_in[:], 0.0)
+        nc.scalar.dma_start(bias_rows_in[0:4, :], bg.rearrange("(c p) -> c p", p=P))
         w4c = keep.tile([P, 2, 2 * N], U8, name="w4c", align_bytes=64)
         nc.sync.dma_start(w4c[:].bitcast(I32), w4_words.bitcast(I32).rearrange("a p n -> p a n"))
 
@@ -91,10 +97,17 @@ def tile_list_premise_slot_gate_kernel(tc, tab_words, tab_scales, offs, w1, w4_w
                 nc.vector.tensor_copy(g[:], tabs[a][:].indirect(offsets[:, 32 * h : 32 * h + 32]))
                 vw[a, h] = g
 
+        ident = keep.tile([P, P], F32, name="ident")
+        make_identity(nc, ident[:])
+        gain_ps = bank(7, [P, KP], "gain_ps")
+        for t in range(PACK):
+            nc.tensor.transpose(gain_ps[:, t:KP:PACK], gain_rows_in[:, t:KP:PACK], ident[:])
+        gain_sb = keep.tile([P, 2 * PACK], F32, name="gain_sb")
+        nc.scalar.copy(gain_sb[:], gain_ps[:, 0 : 2 * PACK])
+        bias_ps = bank(0, [P, P], "bias_ps")
+        nc.tensor.transpose(bias_ps[:], bias_rows_in[:], ident[:])
         half_bg = keep.tile([P, 4], F32, name="half_bg")
-        nc.scalar.activation(half_bg[:], bg_sb[:], ACT.Copy, scale=0.5)
-        half_gain = keep.tile([P, 2, PACK], F32, name="half_gain")
-        nc.scalar.activation(half_gain[:], gain_sb[:], ACT.Copy, scale=0.5)
+        nc.scalar.activation(half_bg[:], bias_ps[:, 0:4], ACT.Copy, scale=0.5)
 
         def quantize(codes, scales, src):
             nc.vector.quantize_mx(out=codes.bitcast(FP8X4), scales=scales, in_=src)
@@ -113,7 +126,7 @@ def tile_list_premise_slot_gate_kernel(tc, tab_words, tab_scales, offs, w1, w4_w
             nc.vector.tensor_copy(grp.rearrange("p t m j -> p m j t"), raw[:].rearrange("p j (m t) -> p m j t", t=PACK))
 
         def load_w1_halves(a, b):
-            grp = stage.tile([P, PACK, P, PACK], BF16, name="grp", align_bytes=64)
+            grp = ring.tile([P, PACK, P, PACK], BF16, name="grp_11", align_bytes=64, offset=GRP_AT)
             for i in range(2):
                 raw = ring.tile([P, PACK, KP // 2], F32, name="rawh_%d" % i, align_bytes=64, offset=SLOTS[(2 * b + a) % 3] + 4096 * i)
                 c0 = KP * b + (KP // 2) * i
@@ -131,7 +144,7 @@ def tile_list_premise_slot_gate_kernel(tc, tab_words, tab_scales, offs, w1, w4_w
             if a != b:
                 grp = keep.tile([P, PACK, P, PACK], BF16, name="grp_mid", align_bytes=64)
             else:
-                grp = stage.tile([P, PACK, P, PACK], BF16, name="grp", align_bytes=64)
+                grp = ring.tile([P, PACK, P, PACK], BF16, name="grp_00", align_bytes=64, offset=GRP_AT)
             cast_w1(a, b, grp[:])
             codes = keep.tile([P, KP], U32, name="w1c%d%d" % (a, b), align_bytes=64)
             scales = keep.tile([P, KP], U8, name="w1s%d%d" % (a, b), align_bytes=64)
@@ -151,26 +164,26 @@ def tile_list_premise_slot_gate_kernel(tc, tab_words, tab_scales, offs, w1, w4_w
 
         w3c, w3s = {}, {}
 
-        def load_w3(b, shares):
+        def load_w3(b):
             raw = ring.tile([P, PACK, N], F32, name="raw3_%d" % b, align_bytes=64, offset=SLOTS[1 + b])
             nc.sync.dma_start(raw[:], w3[KP * b : KP * (b + 1), :].rearrange("(p j) n -> p j n", j=PACK))
-            grp = stage.tile([P, N, PACK], BF16, name="grp", align_bytes=64)
-            for engine, c0, c1 in shares:
-                copy_on(
-                    engine,
-                    grp[:].rearrange("p (c i) j -> p c j i", i=4)[:, c0:c1],
-                    raw[:].rearrange("p j (c i) -> p c j i", i=4)[:, c0:c1],
-                )
+            if b == 0:
+                grp = keep.tile([P, N, PACK], BF16, name="grp_mid", align_bytes=64)
+            else:
+                grp = ring.tile([P, N, PACK], BF16, name="grp3_1", align_bytes=64, offset=SLOTS[1])
+            for c0, c1 in zip(G_CUTS, G_CUTS[1:]):
+                cols = slice(c0, c1)
+                nc.gpsimd.tensor_scalar(grp[:, cols, :], raw[:, :, cols].rearrange("p j n -> p n j"), 0.5, 0.0, ALU.mult, ALU.add)
             w3c[b] = keep.tile([P, N], U32, name="w3c%d" % b, align_bytes=64)
             w3s[b] = keep.tile([P, N], U8, name="w3s%d" % b, align_bytes=64)
             quantize(w3c[b][:], w3s[b][:], grp[:].rearrange("p n j -> p (n j)"))
 
-        th = keep.tile([P, 4, S], F32, name="th")
+        th = [ring.tile([P, 4, CHUNK], F32, name="th%d" % h, align_bytes=64, offset=TH_AT + 4096 * h) for h in range(4)]
 
         def gate(h):
             cols = slice(HALF * h, HALF * (h + 1))
             for c in range(4):
-                acc = psum_o.tile([P, HALF], F32, name="acc_o")
+                acc = bank(4 + (4 * h + c) % 3, [P, HALF], "gate%d%d" % (h, c))
                 for a in range(2):
                     nc.tensor.matmul_mx(
                         out=acc[:],
@@ -181,10 +194,10 @@ def tile_list_premise_slot_gate_kernel(tc, tab_words, tab_scales, offs, w1, w4_w
                         start=(a == 0),
                         stop=(a == 1),
                     )
-                nc.scalar.activation(th[:, c, cols], acc[:], ACT.Tanh, bias=half_bg[:, c : c + 1], scale=0.5)
+                for i in range(2):
+                    nc.scalar.activation(th[2 * h + i][:, c, :], acc[:, CHUNK * i : CHUNK * (i + 1)], ACT.Tanh, bias=half_bg[:, c : c + 1], scale=0.5)
 
-        hc = [keep.tile([P, S], U32, name="hc%d" % b, align_bytes=64) for b in range(2)]
-        hs = [keep.tile([P, S], U8, name="hs%d" % b, align_bytes=64) for b in range(2)]
+        hc, hs = {}, {}
 
         def first_product(acc, b, t0, j0, n):
             h, loc = divmod(j0, HALF)
@@ -204,67 +217,73 @@ def tile_list_premise_slot_gate_kernel(tc, tab_words, tab_scales, offs, w1, w4_w
                     stop=((a, i) == passes[-1]),
                 )
 
-        def gain_v(b, j0, n, hb):
-            act = work.tile([P, 2, n, 2], F32, name="act", bufs=5)
+        act = {}
+
+        def silu_pairs(b, k):
+            act[b, k] = work.tile([P, 2, CHUNK, 2], F32, name="act", bufs=8)
             for s in range(2):
-                acc = psum_a.tile([P, 2, n], F32, name="acc_a")
-                first_product(acc, b, 2 * s, j0, n)
-                nc.scalar.activation(act[:, s], acc[:].rearrange("p e n -> p n e"), ACT.Silu)
-            nc.vector.tensor_tensor(
-                hb.rearrange("p n (s e) -> p n s e", e=2),
-                act[:].rearrange("p s n e -> p n s e"),
-                half_gain[:, b : b + 1, :].rearrange("p o (s e) -> p o s e", e=2).to_broadcast([P, n, 2, 2]),
+                acc = bank((2 * k + s) % 4, [P, 2, CHUNK], "a%d%d%d" % (b, k, s))
+                first_product(acc, b, 2 * s, CHUNK * k, CHUNK)
+                nc.scalar.activation(act[b, k][:, s], acc[:].rearrange("p e n -> p n e"), ACT.Silu)
+
+        def silu_rows(b, k):
+            act[b, k] = work.tile([P, PACK, CHUNK], F32, name="act", bufs=8)
+            for s in range(2):
+                acc = bank((2 * k + s) % 4, [P, 2, CHUNK], "a%d%d%d" % (b, k, s))
+                first_product(acc, b, 2 * s, CHUNK * k, CHUNK)
+                nc.scalar.activation(act[b, k][:, 2 * s : 2 * s + 2, :], acc[:], ACT.Silu)
+
+        hb = {}
+
+        def new_hb(b, k, at):
+            if at is None:
+                hb[b, k] = work.tile([P, CHUNK, PACK], BF16, name="hb", align_bytes=64, bufs=4)
+            else:
+                hb[b, k] = ring.tile([P, CHUNK, PACK], BF16, name="hb%d_%d" % (b, k), align_bytes=64, offset=at)
+
+        def gain_pairs(engine, factors, b, k, at=None):
+            new_hb(b, k, at)
+            engine.tensor_tensor(
+                hb[b, k][:].rearrange("p n (s e) -> p n s e", e=2),
+                act[b, k][:].rearrange("p s n e -> p n s e"),
+                factors[:, PACK * b : PACK * (b + 1)].rearrange("p (o s e) -> p o s e", o=1, e=2).to_broadcast([P, CHUNK, 2, 2]),
                 ALU.mult,
             )
 
-        def quantize_h(b, j0, n, hb):
-            quantize(hc[b][:, j0 : j0 + n], hs[b][:, j0 : j0 + n], hb.rearrange("p n t -> p (n t)"))
-
-        def hidden_v(b, j0, n):
-            if b == 0:
-                hb = ring.tile([P, n, PACK], BF16, name="hb0_%d" % j0, align_bytes=64, offset=SLOTS[0] + 2 * PACK * j0)
-            else:
-                hb = work.tile([P, n, PACK], BF16, name="hb", align_bytes=64)
-            gain_v(b, j0, n, hb[:])
-            quantize_h(b, j0, n, hb[:])
-
-        def hidden_s(b, j0, n, shares):
-            act = work.tile([P, PACK, n], F32, name="act", bufs=5)
-            per_bank = HALF // n
-            for s in range(PACK // per_bank):
-                acc = psum_a.tile([P, per_bank, n], F32, name="acc_a")
-                first_product(acc, b, per_bank * s, j0, n)
-                nc.scalar.activation(act[:, per_bank * s : per_bank * (s + 1), :], acc[:], ACT.Silu)
-            rows = work.tile([P, PACK, n], BF16, name="rows", align_bytes=64)
+        def gain_rows(b, k):
+            rows = work.tile([P, PACK, CHUNK], BF16, name="rows", align_bytes=64)
             for t in range(PACK):
-                nc.scalar.activation(rows[:, t, :], act[:, t, :], ACT.Copy, scale=half_gain[:, b, t : t + 1])
-            hb = work.tile([P, n, PACK], BF16, name="hb", align_bytes=64)
-            for engine, c0, c1 in shares:
-                copy_on(
-                    engine,
-                    hb[:].rearrange("p (c i) t -> p c t i", i=8)[:, c0:c1],
-                    rows[:].rearrange("p t (c i) -> p c t i", i=8)[:, c0:c1],
-                )
-            quantize(hc[b][:, j0 : j0 + n], hs[b][:, j0 : j0 + n], hb[:].rearrange("p n t -> p (n t)"))
+                nc.scalar.activation(rows[:, t, :], act[b, k][:, t, :], ACT.Copy, scale=gain_sb[:, PACK * b + t : PACK * b + t + 1])
+            new_hb(b, k, None)
+            nc.scalar.copy(
+                hb[b, k][:].rearrange("p (c i) t -> p c t i", i=8),
+                rows[:].rearrange("p t (c i) -> p c t i", i=8),
+            )
+
+        def quantize_h(b, k, at=None):
+            if at is None:
+                hc[b, k] = keep.tile([P, CHUNK], U32, name="hc%d_%d" % (b, k), align_bytes=64)
+            else:
+                hc[b, k] = ring.tile([P, CHUNK], U32, name="hc%d_%d" % (b, k), align_bytes=64, offset=at)
+            hs[b, k] = keep.tile([P, CHUNK], U8, name="hs%d_%d" % (b, k), align_bytes=64)
+            quantize(hc[b, k][:], hs[b, k][:], hb[b, k][:].rearrange("p n t -> p (n t)"))
 
         out_v = out.rearrange("(c p) j -> p c j", p=P)
 
-        def final(j0, n, last=False):
+        def final(j0, n, bank0, order, last=False):
             cols = slice(j0, j0 + n)
             per_bank = HALF // n
             for cc in range(4 // per_bank):
-                acc = psum_o.tile([P, per_bank, n], F32, name="acc_o")
-                passes = [(b, i) for i in range(per_bank) for b in range(2)]
-                if last:
-                    passes = [(b, i) for b in range(2) for i in range(per_bank)]
+                acc = bank(bank0 + cc, [P, per_bank, n], "y%d_%d" % (j0, cc))
+                passes = [(b, i) for b in order for i in range(per_bank)]
                 for b, i in passes:
                     c = per_bank * cc + i
                     nc.tensor.matmul_mx(
                         out=acc[:, i, :],
                         lhsT=w3c[b][:, P * c : P * (c + 1)].bitcast(FP8X4),
                         lhsT_scale=w3s[b][:, P * c : P * (c + 1)],
-                        rhs=hc[b][:, cols].bitcast(FP8X4),
-                        rhs_scale=hs[b][:, cols],
+                        rhs=hc[b, j0 // CHUNK][:].bitcast(FP8X4),
+                        rhs_scale=hs[b, j0 // CHUNK][:],
                         start=((b, i) == passes[0]),
                         stop=((b, i) == passes[-1]),
                     )
@@ -272,12 +291,10 @@ def tile_list_premise_slot_gate_kernel(tc, tab_words, tab_scales, offs, w1, w4_w
                 for i in range(0, per_bank, step):
                     c0 = per_bank * cc + i
                     res = work.tile([P, step, n], F32, name="res", bufs=9)
-                    nc.vector.scalar_tensor_tensor(res[:], th[:, c0 : c0 + step, cols], 1.0, acc[:, i : i + step, :], ALU.add, ALU.mult)
+                    nc.vector.scalar_tensor_tensor(res[:], th[j0 // CHUNK][:, c0 : c0 + step, :], 1.0, acc[:, i : i + step, :], ALU.add, ALU.mult)
                     nc.sync.dma_start(out_v[:, c0 : c0 + step, cols], res[:])
 
-        on_v = [("v", 0, P)]
-        on_s = [("s", 0, P)]
-        idle = psum_a.tile([P, HALF], F32, name="acc_a")
+        idle = bank(1, [P, HALF], "idle")
         for c in range(3):
             nc.tensor.matmul_mx(
                 out=idle[:],
@@ -294,17 +311,31 @@ def tile_list_premise_slot_gate_kernel(tc, tab_words, tab_scales, offs, w1, w4_w
         load_w1(1, 0)
         load_w1(0, 1)
         load_w1_halves(1, 1)
-        hidden_v(0, 0, 256)
-        hidden_v(0, 256, 256)
-        hidden_v(0, 512, 256)
-        hidden_v(0, 768, 256)
-        load_w3(0, on_s)
-        hidden_v(1, 0, 256)
-        load_w3(1, on_s)
-        hidden_v(1, 256, 256)
-        final(0, 256)
-        hidden_s(1, 512, 256, [("v", 0, 32)])
-        final(256, 256)
-        hidden_s(1, 768, 256, [("s", 0, 16), ("v", 16, 32)])
-        final(512, 256)
-        final(768, 256, last=True)
+        for k in range(4):
+            silu_pairs(0, k)
+        silu_pairs(1, 0)
+        silu_pairs(1, 1)
+        silu_rows(1, 2)
+        silu_rows(1, 3)
+        load_w3(0)
+        load_w3(1)
+        gain_pairs(nc.vector, gain_ps, 0, 0, at=GRP_AT)
+        gain_pairs(nc.vector, gain_ps, 0, 1, at=GRP_AT + 2048)
+        quantize_h(0, 0)
+        gain_pairs(nc.vector, gain_ps, 1, 0)
+        quantize_h(0, 1)
+        gain_pairs(nc.vector, gain_ps, 1, 1)
+        quantize_h(1, 0)
+        quantize_h(1, 1)
+        gain_pairs(nc.gpsimd, gain_sb, 0, 2, at=SLOTS[2])
+        gain_pairs(nc.gpsimd, gain_sb, 0, 3, at=SLOTS[2] + 2048)
+        gain_rows(1, 2)
+        gain_rows(1, 3)
+        final(0, 256, 2, (0, 1))
+        quantize_h(0, 2, at=TH_AT)
+        quantize_h(1, 2, at=TH_AT + 1024)
+        final(256, 256, 0, (0, 1))
+        quantize_h(0, 3, at=TH_AT + 4096)
+        quantize_h(1, 3, at=TH_AT + 4096 + 1024)
+        final(512, 256, 2, (0, 1))
+        final(768, 256, 0, (0, 1), last=True)

@@ -24,8 +24,8 @@ HALF = 512
 CHUNK = 256
 BANK_TOK = 128
 SLOTS = (0, 8192, 16384)
-TH_AT = 24576
-GRP_AT = TH_AT + 16384
+GRP_AT = 24576
+SCALE_ROW = ((0, 1), (8, 12))
 G_CUTS = (0, 176, 352, 512)
 
 
@@ -49,15 +49,15 @@ def tile_list_premise_slot_gate_kernel(tc, tab_words, tab_scales, offs, w1, w4_w
         ts32 = tab_scales.bitcast(I32)
         for a in range(2):
             for e in range(2):
-                nc.sync.dma_start(swin32[2 * a + e : P : 16, :], ts32[a, e:16:2, :])
+                nc.sync.dma_start(swin32[SCALE_ROW[a][e] : P : 16, :], ts32[a, e:16:2, :])
 
         w4s = keep.tile([P, 2, N], U8, name="w4s", align_bytes=64)
-        nc.gpsimd.memset(w4s[:].bitcast(I32), 0)
+        nc.vector.memset(w4s[:].bitcast(I32), 0)
         gain_rows_in = keep.tile([P, KP], F32, name="gain_rows_in")
-        nc.gpsimd.memset(gain_rows_in[:], 0.0)
+        nc.vector.memset(gain_rows_in[:], 0.0)
         nc.scalar.dma_start(gain_rows_in[0:2, :], gain.rearrange("(b r) -> b r", b=2))
         bias_rows_in = keep.tile([P, P], F32, name="bias_rows_in")
-        nc.gpsimd.memset(bias_rows_in[:], 0.0)
+        nc.vector.memset(bias_rows_in[:], 0.0)
         nc.scalar.dma_start(bias_rows_in[0:4, :], bg.rearrange("(c p) -> c p", p=P))
         w4c = keep.tile([P, 2, 2 * N], U8, name="w4c", align_bytes=64)
         nc.sync.dma_start(w4c[:].bitcast(I32), w4_words.bitcast(I32).rearrange("a p n -> p a n"))
@@ -86,7 +86,7 @@ def tile_list_premise_slot_gate_kernel(tc, tab_words, tab_scales, offs, w1, w4_w
         sg32 = sg[:].bitcast(I32)
         nc.vector.tensor_copy(vs[0][:].bitcast(I32), sg32)
         for r in range(4):
-            nc.sync.dma_start(vs[1][:].bitcast(I32)[r:P:32, :], sg32[16 * (r // 2) + 2 + r % 2 : P : 32, :])
+            nc.sync.dma_start(vs[1][:].bitcast(I32)[r:P:32, :], sg32[16 * (r // 2) + SCALE_ROW[1][r % 2] : P : 32, :])
         for e in range(2):
             nc.sync.dma_start(vs[0][:].bitcast(I32)[2 + e : P : 32, :], sg32[16 + e : P : 32, :])
 
@@ -98,7 +98,8 @@ def tile_list_premise_slot_gate_kernel(tc, tab_words, tab_scales, offs, w1, w4_w
                 vw[a, h] = g
 
         ident = keep.tile([P, P], F32, name="ident")
-        make_identity(nc, ident[:])
+        nc.vector.memset(ident[:], 0.0)
+        make_identity(nc, ident[:], nomemset=True)
         gain_ps = bank(7, [P, KP], "gain_ps")
         for t in range(PACK):
             nc.tensor.transpose(gain_ps[:, t:KP:PACK], gain_rows_in[:, t:KP:PACK], ident[:])
@@ -142,9 +143,9 @@ def tile_list_premise_slot_gate_kernel(tc, tab_words, tab_scales, offs, w1, w4_w
 
         def load_w1(a, b):
             if a != b:
-                grp = keep.tile([P, PACK, P, PACK], BF16, name="grp_mid", align_bytes=64)
+                grp = ring.tile([P, PACK, P, PACK], BF16, name="grp_%d%d" % (a, b), align_bytes=64, offset=GRP_AT + 4096)
             else:
-                grp = ring.tile([P, PACK, P, PACK], BF16, name="grp_00", align_bytes=64, offset=GRP_AT)
+                grp = ring.tile([P, PACK, P, PACK], BF16, name="grp_%d%d" % (a, b), align_bytes=64, offset=GRP_AT)
             cast_w1(a, b, grp[:])
             codes = keep.tile([P, KP], U32, name="w1c%d%d" % (a, b), align_bytes=64)
             scales = keep.tile([P, KP], U8, name="w1s%d%d" % (a, b), align_bytes=64)
@@ -167,23 +168,23 @@ def tile_list_premise_slot_gate_kernel(tc, tab_words, tab_scales, offs, w1, w4_w
         def load_w3(b):
             raw = ring.tile([P, PACK, N], F32, name="raw3_%d" % b, align_bytes=64, offset=SLOTS[1 + b])
             nc.sync.dma_start(raw[:], w3[KP * b : KP * (b + 1), :].rearrange("(p j) n -> p j n", j=PACK))
-            if b == 0:
-                grp = keep.tile([P, N, PACK], BF16, name="grp_mid", align_bytes=64)
-            else:
-                grp = ring.tile([P, N, PACK], BF16, name="grp3_1", align_bytes=64, offset=SLOTS[1])
-            for c0, c1 in zip(G_CUTS, G_CUTS[1:]):
-                cols = slice(c0, c1)
-                nc.gpsimd.tensor_scalar(grp[:, cols, :], raw[:, :, cols].rearrange("p j n -> p n j"), 0.5, 0.0, ALU.mult, ALU.add)
+            grp = keep.tile([P, N, PACK], BF16, name="grp3_%d" % b, align_bytes=64)
+            nc.scalar.activation(
+                grp[:].rearrange("p (c i) j -> p c j i", i=4),
+                raw[:].rearrange("p j (c i) -> p c j i", i=4),
+                ACT.Copy,
+                scale=0.5,
+            )
             w3c[b] = keep.tile([P, N], U32, name="w3c%d" % b, align_bytes=64)
             w3s[b] = keep.tile([P, N], U8, name="w3s%d" % b, align_bytes=64)
             quantize(w3c[b][:], w3s[b][:], grp[:].rearrange("p n j -> p (n j)"))
 
-        th = [ring.tile([P, 4, CHUNK], F32, name="th%d" % h, align_bytes=64, offset=TH_AT + 4096 * h) for h in range(4)]
+        th = keep.tile([P, 4, S], F32, name="th")
 
         def gate(h):
             cols = slice(HALF * h, HALF * (h + 1))
             for c in range(4):
-                acc = bank(4 + (4 * h + c) % 3, [P, HALF], "gate%d%d" % (h, c))
+                acc = bank(4 + c, [P, HALF], "gate%d%d" % (h, c))
                 for a in range(2):
                     nc.tensor.matmul_mx(
                         out=acc[:],
@@ -194,8 +195,7 @@ def tile_list_premise_slot_gate_kernel(tc, tab_words, tab_scales, offs, w1, w4_w
                         start=(a == 0),
                         stop=(a == 1),
                     )
-                for i in range(2):
-                    nc.scalar.activation(th[2 * h + i][:, c, :], acc[:, CHUNK * i : CHUNK * (i + 1)], ACT.Tanh, bias=half_bg[:, c : c + 1], scale=0.5)
+                nc.scalar.activation(th[:, c, cols], acc[:], ACT.Tanh, bias=half_bg[:, c : c + 1], scale=0.5)
 
         hc, hs = {}, {}
 
@@ -250,15 +250,17 @@ def tile_list_premise_slot_gate_kernel(tc, tab_words, tab_scales, offs, w1, w4_w
                 ALU.mult,
             )
 
-        def gain_rows(b, k):
+        def gain_rows(b, k, shares):
             rows = work.tile([P, PACK, CHUNK], BF16, name="rows", align_bytes=64)
             for t in range(PACK):
                 nc.scalar.activation(rows[:, t, :], act[b, k][:, t, :], ACT.Copy, scale=gain_sb[:, PACK * b + t : PACK * b + t + 1])
             new_hb(b, k, None)
-            nc.scalar.copy(
-                hb[b, k][:].rearrange("p (c i) t -> p c t i", i=8),
-                rows[:].rearrange("p t (c i) -> p c t i", i=8),
-            )
+            for engine, c0, c1 in shares:
+                copy_on(
+                    engine,
+                    hb[b, k][:].rearrange("p (c i) t -> p c t i", i=8)[:, c0:c1],
+                    rows[:].rearrange("p t (c i) -> p c t i", i=8)[:, c0:c1],
+                )
 
         def quantize_h(b, k, at=None):
             if at is None:
@@ -274,7 +276,7 @@ def tile_list_premise_slot_gate_kernel(tc, tab_words, tab_scales, offs, w1, w4_w
             cols = slice(j0, j0 + n)
             per_bank = HALF // n
             for cc in range(4 // per_bank):
-                acc = bank(bank0 + cc, [P, per_bank, n], "y%d_%d" % (j0, cc))
+                acc = bank(bank0[cc], [P, per_bank, n], "y%d_%d" % (j0, cc))
                 passes = [(b, i) for b in order for i in range(per_bank)]
                 for b, i in passes:
                     c = per_bank * cc + i
@@ -291,7 +293,7 @@ def tile_list_premise_slot_gate_kernel(tc, tab_words, tab_scales, offs, w1, w4_w
                 for i in range(0, per_bank, step):
                     c0 = per_bank * cc + i
                     res = work.tile([P, step, n], F32, name="res", bufs=9)
-                    nc.vector.scalar_tensor_tensor(res[:], th[j0 // CHUNK][:, c0 : c0 + step, :], 1.0, acc[:, i : i + step, :], ALU.add, ALU.mult)
+                    nc.vector.scalar_tensor_tensor(res[:], th[:, c0 : c0 + step, cols], 1.0, acc[:, i : i + step, :], ALU.add, ALU.mult)
                     nc.sync.dma_start(out_v[:, c0 : c0 + step, cols], res[:])
 
         idle = bank(1, [P, HALF], "idle")
@@ -310,32 +312,27 @@ def tile_list_premise_slot_gate_kernel(tc, tab_words, tab_scales, offs, w1, w4_w
         gate(1)
         load_w1(1, 0)
         load_w1(0, 1)
-        load_w1_halves(1, 1)
+        load_w1(1, 1)
+        held = (GRP_AT + 4096, SLOTS[0], GRP_AT, GRP_AT + 2048)
         for k in range(4):
             silu_pairs(0, k)
-        silu_pairs(1, 0)
-        silu_pairs(1, 1)
-        silu_rows(1, 2)
-        silu_rows(1, 3)
+            gain_pairs(nc.vector, gain_sb, 0, k, at=held[k])
+            quantize_h(0, k)
         load_w3(0)
-        load_w3(1)
-        gain_pairs(nc.vector, gain_ps, 0, 0, at=GRP_AT)
-        gain_pairs(nc.vector, gain_ps, 0, 1, at=GRP_AT + 2048)
-        quantize_h(0, 0)
-        gain_pairs(nc.vector, gain_ps, 1, 0)
-        quantize_h(0, 1)
-        gain_pairs(nc.vector, gain_ps, 1, 1)
+        silu_pairs(1, 0)
+        gain_pairs(nc.vector, gain_sb, 1, 0)
         quantize_h(1, 0)
+        load_w3(1)
+        silu_pairs(1, 1)
+        gain_pairs(nc.vector, gain_sb, 1, 1)
         quantize_h(1, 1)
-        gain_pairs(nc.gpsimd, gain_sb, 0, 2, at=SLOTS[2])
-        gain_pairs(nc.gpsimd, gain_sb, 0, 3, at=SLOTS[2] + 2048)
-        gain_rows(1, 2)
-        gain_rows(1, 3)
-        final(0, 256, 2, (0, 1))
-        quantize_h(0, 2, at=TH_AT)
-        quantize_h(1, 2, at=TH_AT + 1024)
-        final(256, 256, 0, (0, 1))
-        quantize_h(0, 3, at=TH_AT + 4096)
-        quantize_h(1, 3, at=TH_AT + 4096 + 1024)
-        final(512, 256, 2, (0, 1))
-        final(768, 256, 0, (0, 1), last=True)
+        silu_rows(1, 2)
+        final(0, 256, (4, 5), (0, 1))
+        gain_rows(1, 2, [("v", 0, 32)])
+        quantize_h(1, 2)
+        silu_rows(1, 3)
+        final(256, 256, (6, 7), (0, 1))
+        gain_rows(1, 3, [("s", 0, 16), ("v", 16, 32)])
+        quantize_h(1, 3)
+        final(512, 256, (4, 5), (0, 1))
+        final(768, 256, (6, 7), (0, 1), last=True)

@@ -24,9 +24,10 @@ HALF = 512
 CHUNK = 256
 BANK_TOK = 128
 SLOTS = (0, 8192, 16384)
-GRP_AT = 24576
-SCALE_ROW = ((0, 1), (8, 12))
-G_CUTS = (0, 176, 352, 512)
+HB0_AT = 24576
+GRP11_AT = HB0_AT + 8192 - 64
+GRP3_AT = GRP11_AT + 4096 - 64
+ACT11_AT = 40960
 
 
 def tile_list_premise_slot_gate_kernel(tc, tab_words, tab_scales, offs, w1, w4_words, w4_scales, gain, w3, bg, out):
@@ -49,16 +50,17 @@ def tile_list_premise_slot_gate_kernel(tc, tab_words, tab_scales, offs, w1, w4_w
         ts32 = tab_scales.bitcast(I32)
         for a in range(2):
             for e in range(2):
-                nc.sync.dma_start(swin32[SCALE_ROW[a][e] : P : 16, :], ts32[a, e:16:2, :])
+                nc.sync.dma_start(swin32[2 * a + e : P : 16, :], ts32[a, e:16:2, :])
 
         w4s = keep.tile([P, 2, N], U8, name="w4s", align_bytes=64)
-        nc.vector.memset(w4s[:].bitcast(I32), 0)
+        nc.gpsimd.memset(w4s[:].bitcast(I32), 0)
+        ident = keep.tile([P, P], F32, name="ident")
+        nc.vector.memset(ident[:], 0.0)
+        make_identity(nc, ident[:], nomemset=True)
         gain_rows_in = keep.tile([P, KP], F32, name="gain_rows_in")
         nc.vector.memset(gain_rows_in[:], 0.0)
-        nc.scalar.dma_start(gain_rows_in[0:2, :], gain.rearrange("(b r) -> b r", b=2))
-        bias_rows_in = keep.tile([P, P], F32, name="bias_rows_in")
-        nc.vector.memset(bias_rows_in[:], 0.0)
-        nc.scalar.dma_start(bias_rows_in[0:4, :], bg.rearrange("(c p) -> c p", p=P))
+        nc.gpsimd.dma_start(gain_rows_in[0:2, :], gain.rearrange("(b r) -> b r", b=2))
+        nc.gpsimd.dma_start(gain_rows_in[4:8, 0:P], bg.rearrange("(c p) -> c p", p=P))
         w4c = keep.tile([P, 2, 2 * N], U8, name="w4c", align_bytes=64)
         nc.sync.dma_start(w4c[:].bitcast(I32), w4_words.bitcast(I32).rearrange("a p n -> p a n"))
 
@@ -86,7 +88,7 @@ def tile_list_premise_slot_gate_kernel(tc, tab_words, tab_scales, offs, w1, w4_w
         sg32 = sg[:].bitcast(I32)
         nc.vector.tensor_copy(vs[0][:].bitcast(I32), sg32)
         for r in range(4):
-            nc.sync.dma_start(vs[1][:].bitcast(I32)[r:P:32, :], sg32[16 * (r // 2) + SCALE_ROW[1][r % 2] : P : 32, :])
+            nc.sync.dma_start(vs[1][:].bitcast(I32)[r:P:32, :], sg32[16 * (r // 2) + 2 + r % 2 : P : 32, :])
         for e in range(2):
             nc.sync.dma_start(vs[0][:].bitcast(I32)[2 + e : P : 32, :], sg32[16 + e : P : 32, :])
 
@@ -97,18 +99,15 @@ def tile_list_premise_slot_gate_kernel(tc, tab_words, tab_scales, offs, w1, w4_w
                 nc.vector.tensor_copy(g[:], tabs[a][:].indirect(offsets[:, 32 * h : 32 * h + 32]))
                 vw[a, h] = g
 
-        ident = keep.tile([P, P], F32, name="ident")
-        nc.vector.memset(ident[:], 0.0)
-        make_identity(nc, ident[:], nomemset=True)
         gain_ps = bank(7, [P, KP], "gain_ps")
         for t in range(PACK):
             nc.tensor.transpose(gain_ps[:, t:KP:PACK], gain_rows_in[:, t:KP:PACK], ident[:])
         gain_sb = keep.tile([P, 2 * PACK], F32, name="gain_sb")
         nc.scalar.copy(gain_sb[:], gain_ps[:, 0 : 2 * PACK])
         bias_ps = bank(0, [P, P], "bias_ps")
-        nc.tensor.transpose(bias_ps[:], bias_rows_in[:], ident[:])
+        nc.tensor.transpose(bias_ps[:], gain_rows_in[:, 0:P], ident[:])
         half_bg = keep.tile([P, 4], F32, name="half_bg")
-        nc.scalar.activation(half_bg[:], bias_ps[:, 0:4], ACT.Copy, scale=0.5)
+        nc.scalar.activation(half_bg[:], bias_ps[:, 4:8], ACT.Copy, scale=0.5)
 
         def quantize(codes, scales, src):
             nc.vector.quantize_mx(out=codes.bitcast(FP8X4), scales=scales, in_=src)
@@ -127,7 +126,7 @@ def tile_list_premise_slot_gate_kernel(tc, tab_words, tab_scales, offs, w1, w4_w
             nc.vector.tensor_copy(grp.rearrange("p t m j -> p m j t"), raw[:].rearrange("p j (m t) -> p m j t", t=PACK))
 
         def load_w1_halves(a, b):
-            grp = ring.tile([P, PACK, P, PACK], BF16, name="grp_11", align_bytes=64, offset=GRP_AT)
+            grp = ring.tile([P, PACK, P, PACK], BF16, name="grp_11", align_bytes=64, offset=GRP11_AT)
             for i in range(2):
                 raw = ring.tile([P, PACK, KP // 2], F32, name="rawh_%d" % i, align_bytes=64, offset=SLOTS[(2 * b + a) % 3] + 4096 * i)
                 c0 = KP * b + (KP // 2) * i
@@ -142,49 +141,35 @@ def tile_list_premise_slot_gate_kernel(tc, tab_words, tab_scales, offs, w1, w4_w
             w1c[a, b], w1s[a, b] = codes[:], scales[:]
 
         def load_w1(a, b):
-            if a != b:
-                grp = ring.tile([P, PACK, P, PACK], BF16, name="grp_%d%d" % (a, b), align_bytes=64, offset=GRP_AT + 4096)
-            else:
-                grp = ring.tile([P, PACK, P, PACK], BF16, name="grp_%d%d" % (a, b), align_bytes=64, offset=GRP_AT)
+            grp = keep.tile([P, PACK, P, PACK], BF16, name="grp_mid" if a != b else "grp_00", align_bytes=64)
             cast_w1(a, b, grp[:])
             codes = keep.tile([P, KP], U32, name="w1c%d%d" % (a, b), align_bytes=64)
             scales = keep.tile([P, KP], U8, name="w1s%d%d" % (a, b), align_bytes=64)
             quantize(codes[:], scales[:], grp[:].rearrange("p t m j -> p (t m j)"))
             w1c[a, b], w1s[a, b] = codes[:], scales[:]
 
-        def quantize_w1_pair(b, grp2):
-            codes = keep.tile([P, 2, KP], U32, name="w1c%d" % b, align_bytes=64)
-            scales = keep.tile([P, 2, KP], U8, name="w1s%d" % b, align_bytes=64)
-            quantize(
-                codes[:].rearrange("p a c -> p (a c)"),
-                scales[:].rearrange("p a c -> p (a c)"),
-                grp2[:].rearrange("p a t m j -> p (a t m j)"),
-            )
-            for a in range(2):
-                w1c[a, b], w1s[a, b] = codes[:, a, :], scales[:, a, :]
+        w3c, w3s, w3g = {}, {}, {}
 
-        w3c, w3s = {}, {}
-
-        def load_w3(b):
+        def cast_w3(b):
             raw = ring.tile([P, PACK, N], F32, name="raw3_%d" % b, align_bytes=64, offset=SLOTS[1 + b])
             nc.sync.dma_start(raw[:], w3[KP * b : KP * (b + 1), :].rearrange("(p j) n -> p j n", j=PACK))
-            grp = keep.tile([P, N, PACK], BF16, name="grp3_%d" % b, align_bytes=64)
-            nc.scalar.activation(
-                grp[:].rearrange("p (c i) j -> p c j i", i=4),
-                raw[:].rearrange("p j (c i) -> p c j i", i=4),
-                ACT.Copy,
-                scale=0.5,
-            )
+            if b == 0:
+                w3g[b] = ring.tile([P, N, PACK], BF16, name="grp3_0", align_bytes=64, offset=GRP3_AT)
+            else:
+                w3g[b] = keep.tile([P, N, PACK], BF16, name="grp3_1", align_bytes=64)
+            nc.gpsimd.tensor_scalar(w3g[b][:], raw[:].rearrange("p j n -> p n j"), 0.5, 0.0, ALU.mult, ALU.add)
+
+        def quantize_w3(b):
             w3c[b] = keep.tile([P, N], U32, name="w3c%d" % b, align_bytes=64)
-            w3s[b] = keep.tile([P, N], U8, name="w3s%d" % b, align_bytes=64)
-            quantize(w3c[b][:], w3s[b][:], grp[:].rearrange("p n j -> p (n j)"))
+            w3s[b] = ring.tile([P, N], U8, name="w3s%d" % b, align_bytes=64, offset=ACT11_AT + N * b)
+            quantize(w3c[b][:], w3s[b][:], w3g[b][:].rearrange("p n j -> p (n j)"))
 
         th = keep.tile([P, 4, S], F32, name="th")
 
         def gate(h):
             cols = slice(HALF * h, HALF * (h + 1))
             for c in range(4):
-                acc = bank(4 + c, [P, HALF], "gate%d%d" % (h, c))
+                acc = bank(4 + (4 * h + c) % 3, [P, HALF], "gate%d%d" % (h, c))
                 for a in range(2):
                     nc.tensor.matmul_mx(
                         out=acc[:],
@@ -197,7 +182,6 @@ def tile_list_premise_slot_gate_kernel(tc, tab_words, tab_scales, offs, w1, w4_w
                     )
                 nc.scalar.activation(th[:, c, cols], acc[:], ACT.Tanh, bias=half_bg[:, c : c + 1], scale=0.5)
 
-        hc, hs = {}, {}
 
         def first_product(acc, b, t0, j0, n):
             h, loc = divmod(j0, HALF)
@@ -220,7 +204,10 @@ def tile_list_premise_slot_gate_kernel(tc, tab_words, tab_scales, offs, w1, w4_w
         act = {}
 
         def silu_pairs(b, k):
-            act[b, k] = work.tile([P, 2, CHUNK, 2], F32, name="act", bufs=8)
+            if (b, k) == (1, 1):
+                act[b, k] = ring.tile([P, 2, CHUNK, 2], F32, name="act11", align_bytes=64, offset=ACT11_AT)
+            else:
+                act[b, k] = work.tile([P, 2, CHUNK, 2], F32, name="act", bufs=8)
             for s in range(2):
                 acc = bank((2 * k + s) % 4, [P, 2, CHUNK], "a%d%d%d" % (b, k, s))
                 first_product(acc, b, 2 * s, CHUNK * k, CHUNK)
@@ -233,42 +220,35 @@ def tile_list_premise_slot_gate_kernel(tc, tab_words, tab_scales, offs, w1, w4_w
                 first_product(acc, b, 2 * s, CHUNK * k, CHUNK)
                 nc.scalar.activation(act[b, k][:, 2 * s : 2 * s + 2, :], acc[:], ACT.Silu)
 
-        hb = {}
+        hb = [
+            ring.tile([P, S, PACK], BF16, name="hb0", align_bytes=64, offset=HB0_AT),
+            keep.tile([P, S, PACK], BF16, name="hb1", align_bytes=64),
+        ]
 
-        def new_hb(b, k, at):
-            if at is None:
-                hb[b, k] = work.tile([P, CHUNK, PACK], BF16, name="hb", align_bytes=64, bufs=4)
-            else:
-                hb[b, k] = ring.tile([P, CHUNK, PACK], BF16, name="hb%d_%d" % (b, k), align_bytes=64, offset=at)
-
-        def gain_pairs(engine, factors, b, k, at=None):
-            new_hb(b, k, at)
-            engine.tensor_tensor(
-                hb[b, k][:].rearrange("p n (s e) -> p n s e", e=2),
+        def gain_pairs(b, k):
+            nc.vector.tensor_tensor(
+                hb[b][:, CHUNK * k : CHUNK * (k + 1), :].rearrange("p n (s e) -> p n s e", e=2),
                 act[b, k][:].rearrange("p s n e -> p n s e"),
-                factors[:, PACK * b : PACK * (b + 1)].rearrange("p (o s e) -> p o s e", o=1, e=2).to_broadcast([P, CHUNK, 2, 2]),
+                gain_ps[:, PACK * b : PACK * (b + 1)].rearrange("p (o s e) -> p o s e", o=1, e=2).to_broadcast([P, CHUNK, 2, 2]),
                 ALU.mult,
             )
 
-        def gain_rows(b, k, shares):
+        def gain_rows(b, k):
             rows = work.tile([P, PACK, CHUNK], BF16, name="rows", align_bytes=64)
             for t in range(PACK):
                 nc.scalar.activation(rows[:, t, :], act[b, k][:, t, :], ACT.Copy, scale=gain_sb[:, PACK * b + t : PACK * b + t + 1])
-            new_hb(b, k, None)
-            for engine, c0, c1 in shares:
-                copy_on(
-                    engine,
-                    hb[b, k][:].rearrange("p (c i) t -> p c t i", i=8)[:, c0:c1],
-                    rows[:].rearrange("p t (c i) -> p c t i", i=8)[:, c0:c1],
-                )
+            nc.scalar.copy(
+                hb[b][:, CHUNK * k : CHUNK * (k + 1), :].rearrange("p (c i) t -> p c t i", i=8),
+                rows[:].rearrange("p t (c i) -> p c t i", i=8),
+            )
 
-        def quantize_h(b, k, at=None):
-            if at is None:
-                hc[b, k] = keep.tile([P, CHUNK], U32, name="hc%d_%d" % (b, k), align_bytes=64)
-            else:
-                hc[b, k] = ring.tile([P, CHUNK], U32, name="hc%d_%d" % (b, k), align_bytes=64, offset=at)
-            hs[b, k] = keep.tile([P, CHUNK], U8, name="hs%d_%d" % (b, k), align_bytes=64)
-            quantize(hc[b, k][:], hs[b, k][:], hb[b, k][:].rearrange("p n t -> p (n t)"))
+        hc, hs = {}, {}
+
+        def quantize_h(b, j0, n):
+            if b not in hc:
+                hc[b] = keep.tile([P, S], U32, name="hc%d" % b, align_bytes=64)
+                hs[b] = ring.tile([P, S], U8, name="hs%d" % b, align_bytes=64, offset=ACT11_AT + S * (1 + b))
+            quantize(hc[b][:, j0 : j0 + n], hs[b][:, j0 : j0 + n], hb[b][:, j0 : j0 + n, :].rearrange("p n t -> p (n t)"))
 
         out_v = out.rearrange("(c p) j -> p c j", p=P)
 
@@ -284,8 +264,8 @@ def tile_list_premise_slot_gate_kernel(tc, tab_words, tab_scales, offs, w1, w4_w
                         out=acc[:, i, :],
                         lhsT=w3c[b][:, P * c : P * (c + 1)].bitcast(FP8X4),
                         lhsT_scale=w3s[b][:, P * c : P * (c + 1)],
-                        rhs=hc[b, j0 // CHUNK][:].bitcast(FP8X4),
-                        rhs_scale=hs[b, j0 // CHUNK][:],
+                        rhs=hc[b][:, cols].bitcast(FP8X4),
+                        rhs_scale=hs[b][:, cols],
                         start=((b, i) == passes[0]),
                         stop=((b, i) == passes[-1]),
                     )
@@ -296,7 +276,7 @@ def tile_list_premise_slot_gate_kernel(tc, tab_words, tab_scales, offs, w1, w4_w
                     nc.vector.scalar_tensor_tensor(res[:], th[:, c0 : c0 + step, cols], 1.0, acc[:, i : i + step, :], ALU.add, ALU.mult)
                     nc.sync.dma_start(out_v[:, c0 : c0 + step, cols], res[:])
 
-        idle = bank(1, [P, HALF], "idle")
+        idle = bank(0, [P, HALF], "idle")
         for c in range(3):
             nc.tensor.matmul_mx(
                 out=idle[:],
@@ -312,27 +292,31 @@ def tile_list_premise_slot_gate_kernel(tc, tab_words, tab_scales, offs, w1, w4_w
         gate(1)
         load_w1(1, 0)
         load_w1(0, 1)
-        load_w1(1, 1)
-        held = (GRP_AT + 4096, SLOTS[0], GRP_AT, GRP_AT + 2048)
+        load_w1_halves(1, 1)
+        cast_w3(0)
+        cast_w3(1)
         for k in range(4):
             silu_pairs(0, k)
-            gain_pairs(nc.vector, gain_sb, 0, k, at=held[k])
-            quantize_h(0, k)
-        load_w3(0)
         silu_pairs(1, 0)
-        gain_pairs(nc.vector, gain_sb, 1, 0)
-        quantize_h(1, 0)
-        load_w3(1)
         silu_pairs(1, 1)
-        gain_pairs(nc.vector, gain_sb, 1, 1)
-        quantize_h(1, 1)
         silu_rows(1, 2)
-        final(0, 256, (4, 5), (0, 1))
-        gain_rows(1, 2, [("v", 0, 32)])
-        quantize_h(1, 2)
         silu_rows(1, 3)
+        for k in range(4):
+            gain_pairs(0, k)
+        gain_pairs(1, 0)
+        gain_pairs(1, 1)
+        gain_rows(1, 2)
+        gain_rows(1, 3)
+        quantize_w3(0)
+        quantize_h(0, 0, CHUNK)
+        quantize_w3(1)
+        quantize_h(1, 0, CHUNK)
+        quantize_h(0, CHUNK, CHUNK)
+        quantize_h(1, CHUNK, CHUNK)
+        quantize_h(0, HALF, HALF)
+        final(0, 256, (4, 5), (0, 1))
+        quantize_h(1, 512, CHUNK)
         final(256, 256, (6, 7), (0, 1))
-        gain_rows(1, 3, [("s", 0, 16), ("v", 16, 32)])
-        quantize_h(1, 3)
-        final(512, 256, (4, 5), (0, 1))
-        final(768, 256, (6, 7), (0, 1), last=True)
+        quantize_h(1, 768, CHUNK)
+        final(512, 256, (0, 1), (0, 1))
+        final(768, 256, (2, 3), (0, 1), last=True)

@@ -54,13 +54,15 @@ def tile_list_premise_slot_gate_kernel(tc, tab_words, tab_scales, offs, w1, w4_w
 
         w4s = keep.tile([P, 2, N], U8, name="w4s", align_bytes=64)
         nc.gpsimd.memset(w4s[:].bitcast(I32), 0)
+        gain_rows_in = keep.tile([P, KP], F32, name="gain_rows_in")
+        nc.vector.memset(gain_rows_in[:], 0.0)
+        nc.sync.dma_start(gain_rows_in[0:2, :], gain.rearrange("(b r) -> b r", b=2))
+        bias_rows_in = keep.tile([P, P], F32, name="bias_rows_in")
+        nc.vector.memset(bias_rows_in[:], 0.0)
+        nc.gpsimd.dma_start(bias_rows_in[0:4, :], bg.rearrange("(c p) -> c p", p=P))
         ident = keep.tile([P, P], F32, name="ident")
         nc.vector.memset(ident[:], 0.0)
         make_identity(nc, ident[:], nomemset=True)
-        gain_rows_in = keep.tile([P, KP], F32, name="gain_rows_in")
-        nc.vector.memset(gain_rows_in[:], 0.0)
-        nc.gpsimd.dma_start(gain_rows_in[0:2, :], gain.rearrange("(b r) -> b r", b=2))
-        nc.gpsimd.dma_start(gain_rows_in[4:8, 0:P], bg.rearrange("(c p) -> c p", p=P))
         w4c = keep.tile([P, 2, 2 * N], U8, name="w4c", align_bytes=64)
         nc.sync.dma_start(w4c[:].bitcast(I32), w4_words.bitcast(I32).rearrange("a p n -> p a n"))
 
@@ -105,9 +107,9 @@ def tile_list_premise_slot_gate_kernel(tc, tab_words, tab_scales, offs, w1, w4_w
         gain_sb = keep.tile([P, 2 * PACK], F32, name="gain_sb")
         nc.scalar.copy(gain_sb[:], gain_ps[:, 0 : 2 * PACK])
         bias_ps = bank(0, [P, P], "bias_ps")
-        nc.tensor.transpose(bias_ps[:], gain_rows_in[:, 0:P], ident[:])
+        nc.tensor.transpose(bias_ps[:], bias_rows_in[:], ident[:])
         half_bg = keep.tile([P, 4], F32, name="half_bg")
-        nc.scalar.activation(half_bg[:], bias_ps[:, 4:8], ACT.Copy, scale=0.5)
+        nc.scalar.activation(half_bg[:], bias_ps[:, 0:4], ACT.Copy, scale=0.5)
 
         def quantize(codes, scales, src):
             nc.vector.quantize_mx(out=codes.bitcast(FP8X4), scales=scales, in_=src)
@@ -161,7 +163,7 @@ def tile_list_premise_slot_gate_kernel(tc, tab_words, tab_scales, offs, w1, w4_w
 
         def quantize_w3(b):
             w3c[b] = keep.tile([P, N], U32, name="w3c%d" % b, align_bytes=64)
-            w3s[b] = ring.tile([P, N], U8, name="w3s%d" % b, align_bytes=64, offset=ACT11_AT + N * b)
+            w3s[b] = ring.tile([P, N], U8, name="w3s%d" % b, align_bytes=64, offset=ACT11_AT - 64 + N * b)
             quantize(w3c[b][:], w3s[b][:], w3g[b][:].rearrange("p n j -> p (n j)"))
 
         th = keep.tile([P, 4, S], F32, name="th")
@@ -204,10 +206,7 @@ def tile_list_premise_slot_gate_kernel(tc, tab_words, tab_scales, offs, w1, w4_w
         act = {}
 
         def silu_pairs(b, k):
-            if (b, k) == (1, 1):
-                act[b, k] = ring.tile([P, 2, CHUNK, 2], F32, name="act11", align_bytes=64, offset=ACT11_AT)
-            else:
-                act[b, k] = work.tile([P, 2, CHUNK, 2], F32, name="act", bufs=8)
+            act[b, k] = work.tile([P, 2, CHUNK, 2], F32, name="act", bufs=8)
             for s in range(2):
                 acc = bank((2 * k + s) % 4, [P, 2, CHUNK], "a%d%d%d" % (b, k, s))
                 first_product(acc, b, 2 * s, CHUNK * k, CHUNK)
@@ -220,35 +219,61 @@ def tile_list_premise_slot_gate_kernel(tc, tab_words, tab_scales, offs, w1, w4_w
                 first_product(acc, b, 2 * s, CHUNK * k, CHUNK)
                 nc.scalar.activation(act[b, k][:, 2 * s : 2 * s + 2, :], acc[:], ACT.Silu)
 
+        def silu_shared():
+            act["v"] = ring.tile([P, P, PACK], F32, name="act11", align_bytes=64, offset=ACT11_AT)
+            acc = bank(2, [P, PACK, P], "a11v")
+            first_product(acc, 1, 0, CHUNK, P)
+            nc.scalar.activation(act["v"][:], acc[:].rearrange("p t n -> p n t"), ACT.Silu)
+            act["s"] = keep.tile([P, PACK, P], F32, name="act11s")
+            acc = bank(3, [P, PACK, P], "a11s")
+            first_product(acc, 1, 0, CHUNK + P, P)
+            nc.scalar.activation(act["s"][:], acc[:], ACT.Silu)
+
         hb = [
             ring.tile([P, S, PACK], BF16, name="hb0", align_bytes=64, offset=HB0_AT),
             keep.tile([P, S, PACK], BF16, name="hb1", align_bytes=64),
         ]
+        hb00 = ring.tile([P, CHUNK, PACK], BF16, name="hb00", align_bytes=64, offset=SLOTS[0] + 4096)
+
+        apart = {(0, 0): hb00}
+
+        def hb_of(b, j0, n):
+            return apart[b, j0][:] if (b, j0) in apart else hb[b][:, j0 : j0 + n, :]
 
         def gain_pairs(b, k):
             nc.vector.tensor_tensor(
-                hb[b][:, CHUNK * k : CHUNK * (k + 1), :].rearrange("p n (s e) -> p n s e", e=2),
+                hb_of(b, CHUNK * k, CHUNK).rearrange("p n (s e) -> p n s e", e=2),
                 act[b, k][:].rearrange("p s n e -> p n s e"),
                 gain_ps[:, PACK * b : PACK * (b + 1)].rearrange("p (o s e) -> p o s e", o=1, e=2).to_broadcast([P, CHUNK, 2, 2]),
                 ALU.mult,
             )
 
-        def gain_rows(b, k):
-            rows = work.tile([P, PACK, CHUNK], BF16, name="rows", align_bytes=64)
-            for t in range(PACK):
-                nc.scalar.activation(rows[:, t, :], act[b, k][:, t, :], ACT.Copy, scale=gain_sb[:, PACK * b + t : PACK * b + t + 1])
-            nc.scalar.copy(
-                hb[b][:, CHUNK * k : CHUNK * (k + 1), :].rearrange("p (c i) t -> p c t i", i=8),
-                rows[:].rearrange("p t (c i) -> p c t i", i=8),
+        def gain_shared():
+            nc.vector.tensor_tensor(
+                hb[1][:, CHUNK : CHUNK + P, :],
+                act["v"][:],
+                gain_ps[:, PACK : 2 * PACK].rearrange("p (o t) -> p o t", o=1).to_broadcast([P, P, PACK]),
+                ALU.mult,
             )
+
+        def gain_rows(src, j0, n, weave=True):
+            rows = work.tile([P, PACK, n], BF16, name="rows", align_bytes=64)
+            for t in range(PACK):
+                nc.scalar.activation(rows[:, t, :], src[:, t, :], ACT.Copy, scale=gain_sb[:, PACK + t : PACK + t + 1])
+            if weave:
+                nc.scalar.copy(
+                    hb[1][:, j0 : j0 + n, :].rearrange("p (c i) t -> p c t i", i=8),
+                    rows[:].rearrange("p t (c i) -> p c t i", i=8),
+                )
+            return rows
 
         hc, hs = {}, {}
 
         def quantize_h(b, j0, n):
             if b not in hc:
                 hc[b] = keep.tile([P, S], U32, name="hc%d" % b, align_bytes=64)
-                hs[b] = ring.tile([P, S], U8, name="hs%d" % b, align_bytes=64, offset=ACT11_AT + S * (1 + b))
-            quantize(hc[b][:, j0 : j0 + n], hs[b][:, j0 : j0 + n], hb[b][:, j0 : j0 + n, :].rearrange("p n t -> p (n t)"))
+                hs[b] = ring.tile([P, S], U8, name="hs%d" % b, align_bytes=64, offset=ACT11_AT + 960 + S * b)
+            quantize(hc[b][:, j0 : j0 + n], hs[b][:, j0 : j0 + n], hb_of(b, j0, n).rearrange("p n t -> p (n t)"))
 
         out_v = out.rearrange("(c p) j -> p c j", p=P)
 
@@ -298,15 +323,16 @@ def tile_list_premise_slot_gate_kernel(tc, tab_words, tab_scales, offs, w1, w4_w
         for k in range(4):
             silu_pairs(0, k)
         silu_pairs(1, 0)
-        silu_pairs(1, 1)
+        silu_shared()
         silu_rows(1, 2)
         silu_rows(1, 3)
         for k in range(4):
             gain_pairs(0, k)
         gain_pairs(1, 0)
-        gain_pairs(1, 1)
-        gain_rows(1, 2)
-        gain_rows(1, 3)
+        gain_shared()
+        gain_rows(act["s"], CHUNK + P, P)
+        rows12 = gain_rows(act[1, 2], 2 * CHUNK, CHUNK, weave=False)
+        gain_rows(act[1, 3], 3 * CHUNK, CHUNK)
         quantize_w3(0)
         quantize_h(0, 0, CHUNK)
         quantize_w3(1)
@@ -314,6 +340,8 @@ def tile_list_premise_slot_gate_kernel(tc, tab_words, tab_scales, offs, w1, w4_w
         quantize_h(0, CHUNK, CHUNK)
         quantize_h(1, CHUNK, CHUNK)
         quantize_h(0, HALF, HALF)
+        apart[1, 2 * CHUNK] = ring.tile([P, CHUNK, PACK], BF16, name="hb12", align_bytes=64, offset=HB0_AT + 4096)
+        nc.gpsimd.tensor_scalar(apart[1, 2 * CHUNK][:], rows12[:].rearrange("p t n -> p n t"), 1.0, 0.0, ALU.mult, ALU.add)
         final(0, 256, (4, 5), (0, 1))
         quantize_h(1, 512, CHUNK)
         final(256, 256, (6, 7), (0, 1))

@@ -23,11 +23,12 @@ KP = P * PACK
 HALF = 512
 CHUNK = 256
 BANK_TOK = 128
-SLOTS = (0, 8192, 16384)
+SLOTS = (0, 8192, 16384, 45056)
 HB0_AT = 24576
 GRP11_AT = HB0_AT + 8192 - 64
 GRP3_AT = GRP11_AT + 4096 - 64
 ACT11_AT = 40960
+W3_ON_SCALAR = 128
 
 
 def tile_list_premise_slot_gate_kernel(tc, tab_words, tab_scales, offs, w1, w4_words, w4_scales, gain, w3, bg, out):
@@ -44,6 +45,12 @@ def tile_list_premise_slot_gate_kernel(tc, tab_words, tab_scales, offs, w1, w4_w
         offsets = keep.tile([P, S // 16], U16, name="offsets")
         nc.sync.dma_start(offsets[:], offs)
 
+        w4c = keep.tile([P, 2, 2 * N], U8, name="w4c", align_bytes=64)
+        nc.sync.dma_start(w4c[:].bitcast(I32), w4_words.bitcast(I32).rearrange("a p n -> p a n"))
+        early = ring.tile([P, PACK, KP // 2], F32, name="early", align_bytes=64, offset=SLOTS[3])
+        early_src = w1[0:KP, 0 : KP // 2].rearrange("(p j) c -> p j c", j=PACK)
+        nc.sync.dma_start(early[:, 0:2, :], early_src[:, 0:2, :])
+
         swin = ring.tile([P, T], U8, name="swin", align_bytes=64, offset=SLOTS[0])
         swin32 = swin[:].bitcast(I32)
         nc.vector.memset(swin32, 0)
@@ -56,15 +63,12 @@ def tile_list_premise_slot_gate_kernel(tc, tab_words, tab_scales, offs, w1, w4_w
         nc.gpsimd.memset(w4s[:].bitcast(I32), 0)
         gain_rows_in = keep.tile([P, KP], F32, name="gain_rows_in")
         nc.vector.memset(gain_rows_in[:], 0.0)
-        nc.sync.dma_start(gain_rows_in[0:2, :], gain.rearrange("(b r) -> b r", b=2))
         bias_rows_in = keep.tile([P, P], F32, name="bias_rows_in")
         nc.vector.memset(bias_rows_in[:], 0.0)
         nc.gpsimd.dma_start(bias_rows_in[0:4, :], bg.rearrange("(c p) -> c p", p=P))
         ident = keep.tile([P, P], F32, name="ident")
         nc.vector.memset(ident[:], 0.0)
         make_identity(nc, ident[:], nomemset=True)
-        w4c = keep.tile([P, 2, 2 * N], U8, name="w4c", align_bytes=64)
-        nc.sync.dma_start(w4c[:].bitcast(I32), w4_words.bitcast(I32).rearrange("a p n -> p a n"))
 
         tabs = []
 
@@ -74,9 +78,11 @@ def tile_list_premise_slot_gate_kernel(tc, tab_words, tab_scales, offs, w1, w4_w
             tabs.append(tab)
 
         load_tab(0)
+        nc.sync.dma_start(gain_rows_in[0:2, :], gain.rearrange("(b r) -> b r", b=2))
         w4s_src = w4_scales.bitcast(I32).rearrange("a q n -> q a n")
         for d in range(4):
             nc.sync.dma_start(w4s[:].bitcast(I32)[32 * d : 32 * d + 4], w4s_src[4 * d : 4 * d + 4])
+        nc.sync.dma_start(early[:, 2:4, :], early_src[:, 2:4, :])
         load_tab(1)
 
         vs = [keep.tile([P, S], U8, name="vs%d" % a, align_bytes=64) for a in range(2)]
@@ -123,7 +129,7 @@ def tile_list_premise_slot_gate_kernel(tc, tab_words, tab_scales, offs, w1, w4_w
         w1c, w1s = {}, {}
 
         def cast_w1(a, b, grp):
-            raw = ring.tile([P, PACK, KP], F32, name="raw1_%d%d" % (a, b), align_bytes=64, offset=SLOTS[(2 * b + a) % 3])
+            raw = ring.tile([P, PACK, KP], F32, name="raw1_%d%d" % (a, b), align_bytes=64, offset=SLOTS[3 * b])
             nc.sync.dma_start(raw[:], w1[KP * a : KP * (a + 1), KP * b : KP * (b + 1)].rearrange("(p j) c -> p j c", j=PACK))
             nc.vector.tensor_copy(grp.rearrange("p t m j -> p m j t"), raw[:].rearrange("p j (m t) -> p m j t", t=PACK))
 
@@ -150,6 +156,20 @@ def tile_list_premise_slot_gate_kernel(tc, tab_words, tab_scales, offs, w1, w4_w
             quantize(codes[:], scales[:], grp[:].rearrange("p t m j -> p (t m j)"))
             w1c[a, b], w1s[a, b] = codes[:], scales[:]
 
+        def first_blocks():
+            grp0 = keep.tile([P, PACK, P, PACK], BF16, name="grp_00", align_bytes=64)
+            nc.scalar.copy(grp0[:, :, 0:64, :].rearrange("p t m j -> p m j t"), early[:].rearrange("p j (m t) -> p m j t", t=PACK))
+            grp1 = keep.tile([P, PACK, P, PACK], BF16, name="grp_mid", align_bytes=64)
+            cast_w1(1, 0, grp1[:])
+            late = ring.tile([P, PACK, KP // 2], F32, name="late", align_bytes=64, offset=SLOTS[1])
+            nc.sync.dma_start(late[:], w1[0:KP, KP // 2 : KP].rearrange("(p j) c -> p j c", j=PACK))
+            nc.vector.tensor_copy(grp0[:, :, 64:P, :].rearrange("p t m j -> p m j t"), late[:].rearrange("p j (m t) -> p m j t", t=PACK))
+            for a, grp in ((1, grp1), (0, grp0)):
+                codes = keep.tile([P, KP], U32, name="w1c%d0" % a, align_bytes=64)
+                scales = keep.tile([P, KP], U8, name="w1s%d0" % a, align_bytes=64)
+                quantize(codes[:], scales[:], grp[:].rearrange("p t m j -> p (t m j)"))
+                w1c[a, 0], w1s[a, 0] = codes[:], scales[:]
+
         w3c, w3s, w3g = {}, {}, {}
 
         def cast_w3(b):
@@ -159,7 +179,18 @@ def tile_list_premise_slot_gate_kernel(tc, tab_words, tab_scales, offs, w1, w4_w
                 w3g[b] = ring.tile([P, N, PACK], BF16, name="grp3_0", align_bytes=64, offset=GRP3_AT)
             else:
                 w3g[b] = keep.tile([P, N, PACK], BF16, name="grp3_1", align_bytes=64)
-            nc.gpsimd.tensor_scalar(w3g[b][:], raw[:].rearrange("p j n -> p n j"), 0.5, 0.0, ALU.mult, ALU.add)
+            cols = slice(0, N - W3_ON_SCALAR * b)
+            nc.gpsimd.tensor_scalar(w3g[b][:, cols, :], raw[:, :, cols].rearrange("p j n -> p n j"), 0.5, 0.0, ALU.mult, ALU.add)
+            return raw
+
+        def cast_w3_rest(raw):
+            cols = slice(N - W3_ON_SCALAR, N)
+            nc.scalar.activation(
+                w3g[1][:, cols, :].rearrange("p (c i) j -> p c j i", i=4),
+                raw[:, :, cols].rearrange("p j (c i) -> p c j i", i=4),
+                ACT.Copy,
+                scale=0.5,
+            )
 
         def quantize_w3(b):
             w3c[b] = keep.tile([P, N], U32, name="w3c%d" % b, align_bytes=64)
@@ -188,7 +219,7 @@ def tile_list_premise_slot_gate_kernel(tc, tab_words, tab_scales, offs, w1, w4_w
         def first_product(acc, b, t0, j0, n):
             h, loc = divmod(j0, HALF)
             slices = acc.shape[1]
-            passes = [(a, i) for a in range(2) for i in range(slices)]
+            passes = [(a, i) for a in (1, 0) for i in range(slices)]
             if b == 1:
                 passes = [(a, i) for i in range(slices) for a in range(2)]
             for a, i in passes:
@@ -313,26 +344,29 @@ def tile_list_premise_slot_gate_kernel(tc, tab_words, tab_scales, offs, w1, w4_w
                 stop=True,
             )
         gate(0)
-        load_w1(0, 0)
         gate(1)
-        load_w1(1, 0)
+        first_blocks()
         load_w1(0, 1)
         load_w1_halves(1, 1)
         cast_w3(0)
-        cast_w3(1)
+        raw31 = cast_w3(1)
         for k in range(4):
             silu_pairs(0, k)
         silu_pairs(1, 0)
         silu_shared()
-        silu_rows(1, 2)
-        silu_rows(1, 3)
         for k in range(4):
             gain_pairs(0, k)
         gain_pairs(1, 0)
         gain_shared()
+        cast_w3_rest(raw31)
         gain_rows(act["s"], CHUNK + P, P)
+        silu_rows(1, 2)
         rows12 = gain_rows(act[1, 2], 2 * CHUNK, CHUNK, weave=False)
-        gain_rows(act[1, 3], 3 * CHUNK, CHUNK)
+        silu_rows(1, 3)
+        rows13 = gain_rows(act[1, 3], 3 * CHUNK, CHUNK, weave=False)
+        woven13 = hb[1][:, 3 * CHUNK : S, :].rearrange("p (c i) t -> p c t i", i=8)
+        rows13_v = rows13[:].rearrange("p t (c i) -> p c t i", i=8)
+        nc.scalar.copy(woven13[:, 0:16], rows13_v[:, 0:16])
         quantize_w3(0)
         quantize_h(0, 0, CHUNK)
         quantize_w3(1)
@@ -345,6 +379,7 @@ def tile_list_premise_slot_gate_kernel(tc, tab_words, tab_scales, offs, w1, w4_w
         final(0, 256, (4, 5), (0, 1))
         quantize_h(1, 512, CHUNK)
         final(256, 256, (6, 7), (0, 1))
+        nc.vector.tensor_copy(woven13[:, 16:32], rows13_v[:, 16:32])
         quantize_h(1, 768, CHUNK)
         final(512, 256, (0, 1), (0, 1))
         final(768, 256, (2, 3), (0, 1), last=True)

@@ -23,12 +23,12 @@ KP = P * PACK
 HALF = 512
 CHUNK = 256
 BANK_TOK = 128
-SLOTS = (0, 8192, 16384, 45056)
+SLOTS = (0, 8192, 16384)
 HB0_AT = 24576
 GRP11_AT = HB0_AT + 8192 - 64
 GRP3_AT = GRP11_AT + 4096 - 64
 ACT11_AT = 40960
-W3_ON_SCALAR = 128
+W3_ON_SCALAR = 256
 
 
 def tile_list_premise_slot_gate_kernel(tc, tab_words, tab_scales, offs, w1, w4_words, w4_scales, gain, w3, bg, out):
@@ -45,12 +45,6 @@ def tile_list_premise_slot_gate_kernel(tc, tab_words, tab_scales, offs, w1, w4_w
         offsets = keep.tile([P, S // 16], U16, name="offsets")
         nc.sync.dma_start(offsets[:], offs)
 
-        w4c = keep.tile([P, 2, 2 * N], U8, name="w4c", align_bytes=64)
-        nc.sync.dma_start(w4c[:].bitcast(I32), w4_words.bitcast(I32).rearrange("a p n -> p a n"))
-        early = ring.tile([P, PACK, KP // 2], F32, name="early", align_bytes=64, offset=SLOTS[3])
-        early_src = w1[0:KP, 0 : KP // 2].rearrange("(p j) c -> p j c", j=PACK)
-        nc.sync.dma_start(early[:, 0:2, :], early_src[:, 0:2, :])
-
         swin = ring.tile([P, T], U8, name="swin", align_bytes=64, offset=SLOTS[0])
         swin32 = swin[:].bitcast(I32)
         nc.vector.memset(swin32, 0)
@@ -63,12 +57,15 @@ def tile_list_premise_slot_gate_kernel(tc, tab_words, tab_scales, offs, w1, w4_w
         nc.gpsimd.memset(w4s[:].bitcast(I32), 0)
         gain_rows_in = keep.tile([P, KP], F32, name="gain_rows_in")
         nc.vector.memset(gain_rows_in[:], 0.0)
+        nc.sync.dma_start(gain_rows_in[0:2, :], gain.rearrange("(b r) -> b r", b=2))
         bias_rows_in = keep.tile([P, P], F32, name="bias_rows_in")
         nc.vector.memset(bias_rows_in[:], 0.0)
         nc.gpsimd.dma_start(bias_rows_in[0:4, :], bg.rearrange("(c p) -> c p", p=P))
         ident = keep.tile([P, P], F32, name="ident")
         nc.vector.memset(ident[:], 0.0)
         make_identity(nc, ident[:], nomemset=True)
+        w4c = keep.tile([P, 2, 2 * N], U8, name="w4c", align_bytes=64)
+        nc.sync.dma_start(w4c[:].bitcast(I32), w4_words.bitcast(I32).rearrange("a p n -> p a n"))
 
         tabs = []
 
@@ -78,11 +75,9 @@ def tile_list_premise_slot_gate_kernel(tc, tab_words, tab_scales, offs, w1, w4_w
             tabs.append(tab)
 
         load_tab(0)
-        nc.sync.dma_start(gain_rows_in[0:2, :], gain.rearrange("(b r) -> b r", b=2))
         w4s_src = w4_scales.bitcast(I32).rearrange("a q n -> q a n")
         for d in range(4):
             nc.sync.dma_start(w4s[:].bitcast(I32)[32 * d : 32 * d + 4], w4s_src[4 * d : 4 * d + 4])
-        nc.sync.dma_start(early[:, 2:4, :], early_src[:, 2:4, :])
         load_tab(1)
 
         vs = [keep.tile([P, S], U8, name="vs%d" % a, align_bytes=64) for a in range(2)]
@@ -129,7 +124,7 @@ def tile_list_premise_slot_gate_kernel(tc, tab_words, tab_scales, offs, w1, w4_w
         w1c, w1s = {}, {}
 
         def cast_w1(a, b, grp):
-            raw = ring.tile([P, PACK, KP], F32, name="raw1_%d%d" % (a, b), align_bytes=64, offset=SLOTS[3 * b])
+            raw = ring.tile([P, PACK, KP], F32, name="raw1_%d%d" % (a, b), align_bytes=64, offset=SLOTS[(2 * b + a) % 3])
             nc.sync.dma_start(raw[:], w1[KP * a : KP * (a + 1), KP * b : KP * (b + 1)].rearrange("(p j) c -> p j c", j=PACK))
             nc.vector.tensor_copy(grp.rearrange("p t m j -> p m j t"), raw[:].rearrange("p j (m t) -> p m j t", t=PACK))
 
@@ -155,20 +150,6 @@ def tile_list_premise_slot_gate_kernel(tc, tab_words, tab_scales, offs, w1, w4_w
             scales = keep.tile([P, KP], U8, name="w1s%d%d" % (a, b), align_bytes=64)
             quantize(codes[:], scales[:], grp[:].rearrange("p t m j -> p (t m j)"))
             w1c[a, b], w1s[a, b] = codes[:], scales[:]
-
-        def first_blocks():
-            grp0 = keep.tile([P, PACK, P, PACK], BF16, name="grp_00", align_bytes=64)
-            nc.scalar.copy(grp0[:, :, 0:64, :].rearrange("p t m j -> p m j t"), early[:].rearrange("p j (m t) -> p m j t", t=PACK))
-            grp1 = keep.tile([P, PACK, P, PACK], BF16, name="grp_mid", align_bytes=64)
-            cast_w1(1, 0, grp1[:])
-            late = ring.tile([P, PACK, KP // 2], F32, name="late", align_bytes=64, offset=SLOTS[1])
-            nc.sync.dma_start(late[:], w1[0:KP, KP // 2 : KP].rearrange("(p j) c -> p j c", j=PACK))
-            nc.vector.tensor_copy(grp0[:, :, 64:P, :].rearrange("p t m j -> p m j t"), late[:].rearrange("p j (m t) -> p m j t", t=PACK))
-            for a, grp in ((1, grp1), (0, grp0)):
-                codes = keep.tile([P, KP], U32, name="w1c%d0" % a, align_bytes=64)
-                scales = keep.tile([P, KP], U8, name="w1s%d0" % a, align_bytes=64)
-                quantize(codes[:], scales[:], grp[:].rearrange("p t m j -> p (t m j)"))
-                w1c[a, 0], w1s[a, 0] = codes[:], scales[:]
 
         w3c, w3s, w3g = {}, {}, {}
 
@@ -219,7 +200,7 @@ def tile_list_premise_slot_gate_kernel(tc, tab_words, tab_scales, offs, w1, w4_w
         def first_product(acc, b, t0, j0, n):
             h, loc = divmod(j0, HALF)
             slices = acc.shape[1]
-            passes = [(a, i) for a in (1, 0) for i in range(slices)]
+            passes = [(a, i) for a in range(2) for i in range(slices)]
             if b == 1:
                 passes = [(a, i) for i in range(slices) for a in range(2)]
             for a, i in passes:
@@ -344,8 +325,9 @@ def tile_list_premise_slot_gate_kernel(tc, tab_words, tab_scales, offs, w1, w4_w
                 stop=True,
             )
         gate(0)
+        load_w1(0, 0)
         gate(1)
-        first_blocks()
+        load_w1(1, 0)
         load_w1(0, 1)
         load_w1_halves(1, 1)
         cast_w3(0)

@@ -218,7 +218,10 @@ def tile_list_premise_slot_gate_kernel(tc, tab_words, tab_scales, offs, w1, w4_w
         act = {}
 
         def silu_pairs(b, k):
-            act[b, k] = work.tile([P, 2, CHUNK, 2], F32, name="act", bufs=8)
+            if b == 1:
+                act[b, k] = ring.tile([P, 2, CHUNK, 2], F32, name="act10", align_bytes=64, offset=ACT11_AT)
+            else:
+                act[b, k] = work.tile([P, 2, CHUNK, 2], F32, name="act", bufs=8)
             for s in range(2):
                 acc = bank((2 * k + s) % 4, [P, 2, CHUNK], "a%d%d%d" % (b, k, s))
                 first_product(acc, b, 2 * s, CHUNK * k, CHUNK)
@@ -232,7 +235,7 @@ def tile_list_premise_slot_gate_kernel(tc, tab_words, tab_scales, offs, w1, w4_w
                 nc.scalar.activation(act[b, k][:, 2 * s : 2 * s + 2, :], acc[:], ACT.Silu)
 
         def silu_shared():
-            act["v"] = ring.tile([P, P, PACK], F32, name="act11", align_bytes=64, offset=ACT11_AT)
+            act["v"] = keep.tile([P, P, PACK], F32, name="act11")
             acc = bank(2, [P, PACK, P], "a11v")
             first_product(acc, 1, 0, CHUNK, P)
             nc.scalar.activation(act["v"][:], acc[:].rearrange("p t n -> p n t"), ACT.Silu)
@@ -245,11 +248,13 @@ def tile_list_premise_slot_gate_kernel(tc, tab_words, tab_scales, offs, w1, w4_w
             ring.tile([P, S, PACK], BF16, name="hb0", align_bytes=64, offset=HB0_AT),
             keep.tile([P, S, PACK], BF16, name="hb1", align_bytes=64),
         ]
-        hb00 = ring.tile([P, CHUNK, PACK], BF16, name="hb00", align_bytes=64, offset=SLOTS[0] + 4096)
+        hb0_first = ring.tile([P, HALF, PACK], BF16, name="hb0_first", align_bytes=64, offset=SLOTS[0] + 4096)
 
-        apart = {(0, 0): hb00}
+        apart = {}
 
         def hb_of(b, j0, n):
+            if b == 0 and j0 < HALF:
+                return hb0_first[:, j0 : j0 + n, :]
             return apart[b, j0][:] if (b, j0) in apart else hb[b][:, j0 : j0 + n, :]
 
         def gain_pairs(b, k):
@@ -289,29 +294,32 @@ def tile_list_premise_slot_gate_kernel(tc, tab_words, tab_scales, offs, w1, w4_w
 
         out_v = out.rearrange("(c p) j -> p c j", p=P)
 
-        def final(j0, n, bank0, order, last=False):
-            cols = slice(j0, j0 + n)
-            per_bank = HALF // n
-            for cc in range(4 // per_bank):
-                acc = bank(bank0[cc], [P, per_bank, n], "y%d_%d" % (j0, cc))
-                passes = [(b, i) for b in order for i in range(per_bank)]
-                for b, i in passes:
-                    c = per_bank * cc + i
+        y = {}
+
+        def third_product(k, b, banks):
+            cols = slice(CHUNK * k, CHUNK * (k + 1))
+            for cc in range(2):
+                if b == 0:
+                    y[k, cc] = bank(banks[cc], [P, 2, CHUNK], "y%d%d" % (k, cc))
+                for i in range(2):
+                    c = 2 * cc + i
                     nc.tensor.matmul_mx(
-                        out=acc[:, i, :],
+                        out=y[k, cc][:, i, :],
                         lhsT=w3c[b][:, P * c : P * (c + 1)].bitcast(FP8X4),
                         lhsT_scale=w3s[b][:, P * c : P * (c + 1)],
                         rhs=hc[b][:, cols].bitcast(FP8X4),
                         rhs_scale=hs[b][:, cols],
-                        start=((b, i) == passes[0]),
-                        stop=((b, i) == passes[-1]),
+                        start=(b == 0 and i == 0),
+                        stop=(b == 1 and i == 1),
                     )
-                step = 1 if last and cc == 4 // per_bank - 1 else per_bank
-                for i in range(0, per_bank, step):
-                    c0 = per_bank * cc + i
-                    res = work.tile([P, step, n], F32, name="res", bufs=9)
-                    nc.vector.scalar_tensor_tensor(res[:], th[:, c0 : c0 + step, cols], 1.0, acc[:, i : i + step, :], ALU.add, ALU.mult)
-                    nc.sync.dma_start(out_v[:, c0 : c0 + step, cols], res[:])
+
+        def gated_store(k, cc, step=2):
+            cols = slice(CHUNK * k, CHUNK * (k + 1))
+            for i in range(0, 2, step):
+                c0 = 2 * cc + i
+                res = work.tile([P, step, CHUNK], F32, name="res", bufs=9)
+                nc.vector.scalar_tensor_tensor(res[:], th[:, c0 : c0 + step, cols], 1.0, y[k, cc][:, i : i + step, :], ALU.add, ALU.mult)
+                nc.sync.dma_start(out_v[:, c0 : c0 + step, cols], res[:])
 
         idle = bank(0, [P, HALF], "idle")
         for c in range(3):
@@ -358,10 +366,22 @@ def tile_list_premise_slot_gate_kernel(tc, tab_words, tab_scales, offs, w1, w4_w
         quantize_h(0, HALF, HALF)
         apart[1, 2 * CHUNK] = ring.tile([P, CHUNK, PACK], BF16, name="hb12", align_bytes=64, offset=HB0_AT + 4096)
         nc.gpsimd.tensor_scalar(apart[1, 2 * CHUNK][:], rows12[:].rearrange("p t n -> p n t"), 1.0, 0.0, ALU.mult, ALU.add)
-        final(0, 256, (4, 5), (0, 1))
-        quantize_h(1, 512, CHUNK)
-        final(256, 256, (6, 7), (0, 1))
+        third_product(0, 0, (4, 5))
+        third_product(0, 1, (4, 5))
+        gated_store(0, 0)
+        gated_store(0, 1)
+        quantize_h(1, 2 * CHUNK, CHUNK)
+        third_product(1, 0, (6, 7))
+        third_product(1, 1, (6, 7))
+        third_product(2, 0, (0, 1))
+        third_product(2, 1, (0, 1))
+        third_product(3, 0, (2, 3))
+        gated_store(1, 0)
+        gated_store(1, 1)
         nc.vector.tensor_copy(woven13[:, 16:32], rows13_v[:, 16:32])
-        quantize_h(1, 768, CHUNK)
-        final(512, 256, (0, 1), (0, 1))
-        final(768, 256, (2, 3), (0, 1), last=True)
+        gated_store(2, 0)
+        quantize_h(1, 3 * CHUNK, CHUNK)
+        third_product(3, 1, (2, 3))
+        gated_store(2, 1)
+        gated_store(3, 0)
+        gated_store(3, 1, step=1)

from contextlib import ExitStack

import concourse.mybir as mybir
from concourse.masks import make_identity

K, T, S, H, N = 1024, 2048, 1024, 1024, 512
FLOPS = 2 * S * (K * H + K * N + H * N)

F32 = mybir.dt.float32
BF16 = mybir.dt.bfloat16
I32 = mybir.dt.int32
U32 = mybir.dt.uint32
U16 = mybir.dt.uint16
U8 = mybir.dt.uint8
FP8X4 = mybir.dt.float8_e4m3fn_x4
FP4X4 = mybir.dt.float4_e2m1fn_x4
ACT = mybir.ActivationFunctionType
ALU = mybir.AluOpType

P = 128
PACK = 4
KP = P * PACK
HALF = 512
CHUNK = 256
BANK_TOK = 128
SLOTS = (0, 8192, 16384)
HB0_AT = 24576
GRP11_AT = HB0_AT + 8192 - 64
GRP3_AT = GRP11_AT + 4096 - 64
ACT11_AT = 40960
W3_ON_SCALAR = 256


def tile_list_premise_slot_gate_kernel(tc, tab_words, tab_scales, offs, w1, w4_words, w4_scales, gain, w3, bg, out):
    nc = tc.nc
    with ExitStack() as ctx:
        keep = ctx.enter_context(tc.tile_pool(name="keep", bufs=1))
        ring = ctx.enter_context(tc.tile_pool(name="ring", bufs=1))
        work = ctx.enter_context(tc.tile_pool(name="work", bufs=3))
        psum = ctx.enter_context(tc.psum_pool(name="psum", bufs=1))

        def bank(i, shape, name):
            return psum.tile(shape, F32, name=name, offset=2048 * i)

        offsets = keep.tile([P, S // 16], U16, name="offsets")
        nc.sync.dma_start(offsets[:], offs)

        swin = ring.tile([P, T], U8, name="swin", align_bytes=64, offset=SLOTS[0])
        swin32 = swin[:].bitcast(I32)
        nc.vector.memset(swin32, 0)
        ts32 = tab_scales.bitcast(I32)
        for a in range(2):
            for e in range(2):
                nc.sync.dma_start(swin32[2 * a + e : P : 16, :], ts32[a, e:16:2, :])

        w4s = keep.tile([P, 2, N], U8, name="w4s", align_bytes=64)
        nc.gpsimd.memset(w4s[:].bitcast(I32), 0)
        gain_rows_in = keep.tile([P, KP], F32, name="gain_rows_in")
        nc.vector.memset(gain_rows_in[:], 0.0)
        nc.sync.dma_start(gain_rows_in[0:2, :], gain.rearrange("(b r) -> b r", b=2))
        bias_rows_in = keep.tile([P, P], F32, name="bias_rows_in")
        nc.vector.memset(bias_rows_in[:], 0.0)
        nc.gpsimd.dma_start(bias_rows_in[0:4, :], bg.rearrange("(c p) -> c p", p=P))
        ident = keep.tile([P, P], F32, name="ident")
        nc.vector.memset(ident[:], 0.0)
        make_identity(nc, ident[:], nomemset=True)
        w4c = keep.tile([P, 2, 2 * N], U8, name="w4c", align_bytes=64)
        nc.sync.dma_start(w4c[:].bitcast(I32), w4_words.bitcast(I32).rearrange("a p n -> p a n"))

        tabs = []

        def load_tab(a):
            tab = ring.tile([P, T], U32, name="tab%d" % a, align_bytes=64, offset=SLOTS[1 + a])
            nc.sync.dma_start(tab[:].bitcast(I32), tab_words[a].rearrange("p t i -> p (t i)").bitcast(I32))
            tabs.append(tab)

        load_tab(0)
        w4s_src = w4_scales.bitcast(I32).rearrange("a q n -> q a n")
        for d in range(4):
            nc.sync.dma_start(w4s[:].bitcast(I32)[32 * d : 32 * d + 4], w4s_src[4 * d : 4 * d + 4])
        load_tab(1)

        vs = [keep.tile([P, S], U8, name="vs%d" % a, align_bytes=64) for a in range(2)]
        nc.vector.memset(vs[1][:].bitcast(I32), 0)
        warm = keep.tile([P, 2], F32, name="warm")
        nc.vector.memset(warm[:, 0:1], 0.0)
        nc.scalar.activation(warm[:, 1:2], warm[:, 0:1], ACT.Silu)

        sg = keep.tile([P, S], U8, name="sg", align_bytes=64)
        nc.vector.tensor_copy(sg[:], swin[:].indirect(offsets[:]))
        sg32 = sg[:].bitcast(I32)
        nc.vector.tensor_copy(vs[0][:].bitcast(I32), sg32)
        for r in range(4):
            nc.sync.dma_start(vs[1][:].bitcast(I32)[r:P:32, :], sg32[16 * (r // 2) + 2 + r % 2 : P : 32, :])
        for e in range(2):
            nc.sync.dma_start(vs[0][:].bitcast(I32)[2 + e : P : 32, :], sg32[16 + e : P : 32, :])

        vw = {}
        for a in range(2):
            for h in range(2):
                g = keep.tile([P, HALF], U32, name="vw%d%d" % (a, h), align_bytes=64)
                nc.vector.tensor_copy(g[:], tabs[a][:].indirect(offsets[:, 32 * h : 32 * h + 32]))
                vw[a, h] = g

        gain_ps = bank(7, [P, KP], "gain_ps")
        for t in range(PACK):
            nc.tensor.transpose(gain_ps[:, t:KP:PACK], gain_rows_in[:, t:KP:PACK], ident[:])
        gain_sb = keep.tile([P, 2 * PACK], F32, name="gain_sb")
        nc.scalar.copy(gain_sb[:], gain_ps[:, 0 : 2 * PACK])
        bias_ps = bank(0, [P, P], "bias_ps")
        nc.tensor.transpose(bias_ps[:], bias_rows_in[:], ident[:])
        half_bg = keep.tile([P, 4], F32, name="half_bg")
        nc.scalar.activation(half_bg[:], bias_ps[:, 0:4], ACT.Copy, scale=0.5)

        def quantize(codes, scales, src):
            nc.vector.quantize_mx(out=codes.bitcast(FP8X4), scales=scales, in_=src)

        def copy_on(engine, dst, src):
            if engine == "v":
                nc.vector.tensor_copy(dst, src)
            else:
                nc.scalar.copy(dst, src)

        w1c, w1s = {}, {}

        def cast_w1(a, b, grp):
            raw = ring.tile([P, PACK, KP], F32, name="raw1_%d%d" % (a, b), align_bytes=64, offset=SLOTS[(2 * b + a) % 3])
            nc.sync.dma_start(raw[:], w1[KP * a : KP * (a + 1), KP * b : KP * (b + 1)].rearrange("(p j) c -> p j c", j=PACK))
            nc.vector.tensor_copy(grp.rearrange("p t m j -> p m j t"), raw[:].rearrange("p j (m t) -> p m j t", t=PACK))

        def load_w1_halves(a, b):
            grp = ring.tile([P, PACK, P, PACK], BF16, name="grp_11", align_bytes=64, offset=GRP11_AT)
            for i in range(2):
                raw = ring.tile([P, PACK, KP // 2], F32, name="rawh_%d" % i, align_bytes=64, offset=SLOTS[(2 * b + a) % 3] + 4096 * i)
                c0 = KP * b + (KP // 2) * i
                nc.sync.dma_start(raw[:], w1[KP * a : KP * (a + 1), c0 : c0 + KP // 2].rearrange("(p j) c -> p j c", j=PACK))
                nc.vector.tensor_copy(
                    grp[:, :, 64 * i : 64 * (i + 1), :].rearrange("p t m j -> p m j t"),
                    raw[:].rearrange("p j (m t) -> p m j t", t=PACK),
                )
            codes = keep.tile([P, KP], U32, name="w1c%d%d" % (a, b), align_bytes=64)
            scales = keep.tile([P, KP], U8, name="w1s%d%d" % (a, b), align_bytes=64)
            quantize(codes[:], scales[:], grp[:].rearrange("p t m j -> p (t m j)"))
            w1c[a, b], w1s[a, b] = codes[:], scales[:]

        def load_w1(a, b):
            grp = keep.tile([P, PACK, P, PACK], BF16, name="grp_mid" if a != b else "grp_00", align_bytes=64)
            cast_w1(a, b, grp[:])
            codes = keep.tile([P, KP], U32, name="w1c%d%d" % (a, b), align_bytes=64)
            scales = keep.tile([P, KP], U8, name="w1s%d%d" % (a, b), align_bytes=64)
            quantize(codes[:], scales[:], grp[:].rearrange("p t m j -> p (t m j)"))
            w1c[a, b], w1s[a, b] = codes[:], scales[:]

        w3c, w3s, w3g = {}, {}, {}

        def cast_w3(b):
            raw = ring.tile([P, PACK, N], F32, name="raw3_%d" % b, align_bytes=64, offset=SLOTS[1 + b])
            nc.sync.dma_start(raw[:], w3[KP * b : KP * (b + 1), :].rearrange("(p j) n -> p j n", j=PACK))
            if b == 0:
                w3g[b] = ring.tile([P, N, PACK], BF16, name="grp3_0", align_bytes=64, offset=GRP3_AT)
            else:
                w3g[b] = keep.tile([P, N, PACK], BF16, name="grp3_1", align_bytes=64)
            cols = slice(0, N - W3_ON_SCALAR * b)
            nc.gpsimd.tensor_scalar(w3g[b][:, cols, :], raw[:, :, cols].rearrange("p j n -> p n j"), 0.5, 0.0, ALU.mult, ALU.add)
            return raw

        def cast_w3_rest(raw):
            cols = slice(N - W3_ON_SCALAR, N)
            nc.scalar.activation(
                w3g[1][:, cols, :].rearrange("p (c i) j -> p c j i", i=4),
                raw[:, :, cols].rearrange("p j (c i) -> p c j i", i=4),
                ACT.Copy,
                scale=0.5,
            )

        def quantize_w3(b):
            w3c[b] = keep.tile([P, N], U32, name="w3c%d" % b, align_bytes=64)
            w3s[b] = ring.tile([P, N], U8, name="w3s%d" % b, align_bytes=64, offset=ACT11_AT - 64 + N * b)
            quantize(w3c[b][:], w3s[b][:], w3g[b][:].rearrange("p n j -> p (n j)"))

        th = keep.tile([P, 4, S], F32, name="th")

        def gate(h):
            cols = slice(HALF * h, HALF * (h + 1))
            for c in range(4):
                acc = bank(4 + (4 * h + c) % 3, [P, HALF], "gate%d%d" % (h, c))
                for a in range(2):
                    nc.tensor.matmul_mx(
                        out=acc[:],
                        lhsT=w4c[:, a, 2 * P * c : 2 * P * (c + 1)].bitcast(FP4X4),
                        lhsT_scale=w4s[:, a, P * c : P * (c + 1)],
                        rhs=vw[a, h][:].bitcast(FP8X4),
                        rhs_scale=vs[a][:, cols],
                        start=(a == 0),
                        stop=(a == 1),
                    )
                nc.scalar.activation(th[:, c, cols], acc[:], ACT.Tanh, bias=half_bg[:, c : c + 1], scale=0.5)


        def first_product(acc, b, t0, j0, n):
            h, loc = divmod(j0, HALF)
            slices = acc.shape[1]
            passes = [(a, i) for a in range(2) for i in range(slices)]
            if b == 1:
                passes = [(a, i) for i in range(slices) for a in range(2)]
            for a, i in passes:
                t = t0 + i
                nc.tensor.matmul_mx(
                    out=acc[:, i, :],
                    lhsT=w1c[a, b][:, P * t : P * (t + 1)].bitcast(FP8X4),
                    lhsT_scale=w1s[a, b][:, P * t : P * (t + 1)],
                    rhs=vw[a, h][:, loc : loc + n].bitcast(FP8X4),
                    rhs_scale=vs[a][:, j0 : j0 + n],
                    start=((a, i) == passes[0]),
                    stop=((a, i) == passes[-1]),
                )

        act = {}

        def silu_pairs(b, k):
            if b == 1:
                act[b, k] = ring.tile([P, 2, CHUNK, 2], F32, name="act10", align_bytes=64, offset=ACT11_AT)
            else:
                act[b, k] = work.tile([P, 2, CHUNK, 2], F32, name="act", bufs=8)
            for s in range(2):
                acc = bank((2 * k + s) % 4, [P, 2, CHUNK], "a%d%d%d" % (b, k, s))
                first_product(acc, b, 2 * s, CHUNK * k, CHUNK)
                nc.scalar.activation(act[b, k][:, s], acc[:].rearrange("p e n -> p n e"), ACT.Silu)

        def silu_rows(b, k):
            act[b, k] = work.tile([P, PACK, CHUNK], F32, name="act", bufs=8)
            for s in range(2):
                acc = bank((2 * k + s) % 4, [P, 2, CHUNK], "a%d%d%d" % (b, k, s))
                first_product(acc, b, 2 * s, CHUNK * k, CHUNK)
                nc.scalar.activation(act[b, k][:, 2 * s : 2 * s + 2, :], acc[:], ACT.Silu)

        def silu_shared():
            act["v"] = keep.tile([P, P, PACK], F32, name="act11")
            acc = bank(2, [P, PACK, P], "a11v")
            first_product(acc, 1, 0, CHUNK, P)
            nc.scalar.activation(act["v"][:], acc[:].rearrange("p t n -> p n t"), ACT.Silu)
            act["s"] = keep.tile([P, PACK, P], F32, name="act11s")
            acc = bank(3, [P, PACK, P], "a11s")
            first_product(acc, 1, 0, CHUNK + P, P)
            nc.scalar.activation(act["s"][:], acc[:], ACT.Silu)

        hb = [
            ring.tile([P, S, PACK], BF16, name="hb0", align_bytes=64, offset=HB0_AT),
            keep.tile([P, S, PACK], BF16, name="hb1", align_bytes=64),
        ]
        hb0_first = ring.tile([P, HALF, PACK], BF16, name="hb0_first", align_bytes=64, offset=SLOTS[0] + 4096)

        apart = {}

        def hb_of(b, j0, n):
            if b == 0 and j0 < HALF:
                return hb0_first[:, j0 : j0 + n, :]
            return apart[b, j0][:] if (b, j0) in apart else hb[b][:, j0 : j0 + n, :]

        def gain_pairs(b, k):
            nc.vector.tensor_tensor(
                hb_of(b, CHUNK * k, CHUNK).rearrange("p n (s e) -> p n s e", e=2),
                act[b, k][:].rearrange("p s n e -> p n s e"),
                gain_ps[:, PACK * b : PACK * (b + 1)].rearrange("p (o s e) -> p o s e", o=1, e=2).to_broadcast([P, CHUNK, 2, 2]),
                ALU.mult,
            )

        def gain_shared():
            nc.vector.tensor_tensor(
                hb[1][:, CHUNK : CHUNK + P, :],
                act["v"][:],
                gain_ps[:, PACK : 2 * PACK].rearrange("p (o t) -> p o t", o=1).to_broadcast([P, P, PACK]),
                ALU.mult,
            )

        def gain_rows(src, j0, n, weave=True):
            rows = work.tile([P, PACK, n], BF16, name="rows", align_bytes=64)
            for t in range(PACK):
                nc.scalar.activation(rows[:, t, :], src[:, t, :], ACT.Copy, scale=gain_sb[:, PACK + t : PACK + t + 1])
            if weave:
                nc.scalar.copy(
                    hb[1][:, j0 : j0 + n, :].rearrange("p (c i) t -> p c t i", i=8),
                    rows[:].rearrange("p t (c i) -> p c t i", i=8),
                )
            return rows

        hc, hs = {}, {}

        def quantize_h(b, j0, n):
            if b not in hc:
                hc[b] = keep.tile([P, S], U32, name="hc%d" % b, align_bytes=64)
                hs[b] = ring.tile([P, S], U8, name="hs%d" % b, align_bytes=64, offset=ACT11_AT + 960 + S * b)
            quantize(hc[b][:, j0 : j0 + n], hs[b][:, j0 : j0 + n], hb_of(b, j0, n).rearrange("p n t -> p (n t)"))

        out_v = out.rearrange("(c p) j -> p c j", p=P)

        y = {}

        def third_product(k, b, banks):
            cols = slice(CHUNK * k, CHUNK * (k + 1))
            for cc in range(2):
                if b == 0:
                    y[k, cc] = bank(banks[cc], [P, 2, CHUNK], "y%d%d" % (k, cc))
                for i in range(2):
                    c = 2 * cc + i
                    nc.tensor.matmul_mx(
                        out=y[k, cc][:, i, :],
                        lhsT=w3c[b][:, P * c : P * (c + 1)].bitcast(FP8X4),
                        lhsT_scale=w3s[b][:, P * c : P * (c + 1)],
                        rhs=hc[b][:, cols].bitcast(FP8X4),
                        rhs_scale=hs[b][:, cols],
                        start=(b == 0 and i == 0),
                        stop=(b == 1 and i == 1),
                    )

        def gated_store(k, cc, step=2):
            cols = slice(CHUNK * k, CHUNK * (k + 1))
            for i in range(0, 2, step):
                c0 = 2 * cc + i
                res = work.tile([P, step, CHUNK], F32, name="res", bufs=9)
                nc.vector.scalar_tensor_tensor(res[:], th[:, c0 : c0 + step, cols], 1.0, y[k, cc][:, i : i + step, :], ALU.add, ALU.mult)
                nc.sync.dma_start(out_v[:, c0 : c0 + step, cols], res[:])

        idle = bank(0, [P, HALF], "idle")
        for c in range(3):
            nc.tensor.matmul_mx(
                out=idle[:],
                lhsT=w4c[:, 0, 2 * P * c : 2 * P * (c + 1)].bitcast(FP4X4),
                lhsT_scale=w4s[:, 0, P * c : P * (c + 1)],
                rhs=vw[0, 0][:].bitcast(FP8X4),
                rhs_scale=sg[:, 0:HALF],
                start=True,
                stop=True,
            )
        gate(0)
        load_w1(0, 0)
        gate(1)
        load_w1(1, 0)
        load_w1(0, 1)
        load_w1_halves(1, 1)
        cast_w3(0)
        raw31 = cast_w3(1)
        for k in range(4):
            silu_pairs(0, k)
        silu_pairs(1, 0)
        silu_shared()
        for k in range(4):
            gain_pairs(0, k)
        gain_pairs(1, 0)
        gain_shared()
        cast_w3_rest(raw31)
        gain_rows(act["s"], CHUNK + P, P)
        silu_rows(1, 2)
        rows12 = gain_rows(act[1, 2], 2 * CHUNK, CHUNK, weave=False)
        silu_rows(1, 3)
        rows13 = gain_rows(act[1, 3], 3 * CHUNK, CHUNK, weave=False)
        woven13 = hb[1][:, 3 * CHUNK : S, :].rearrange("p (c i) t -> p c t i", i=8)
        rows13_v = rows13[:].rearrange("p t (c i) -> p c t i", i=8)
        nc.scalar.copy(woven13[:, 0:16], rows13_v[:, 0:16])
        quantize_w3(0)
        quantize_h(0, 0, CHUNK)
        quantize_w3(1)
        quantize_h(1, 0, CHUNK)
        quantize_h(0, CHUNK, CHUNK)
        quantize_h(1, CHUNK, CHUNK)
        quantize_h(0, HALF, HALF)
        apart[1, 2 * CHUNK] = ring.tile([P, CHUNK, PACK], BF16, name="hb12", align_bytes=64, offset=HB0_AT + 4096)
        nc.gpsimd.tensor_scalar(apart[1, 2 * CHUNK][:], rows12[:].rearrange("p t n -> p n t"), 1.0, 0.0, ALU.mult, ALU.add)
        third_product(0, 0, (4, 5))
        third_product(0, 1, (4, 5))
        gated_store(0, 0)
        gated_store(0, 1)
        quantize_h(1, 2 * CHUNK, CHUNK)
        third_product(1, 0, (6, 7))
        third_product(1, 1, (6, 7))
        third_product(2, 0, (0, 1))
        third_product(2, 1, (0, 1))
        third_product(3, 0, (2, 3))
        gated_store(1, 0)
        gated_store(1, 1)
        nc.vector.tensor_copy(woven13[:, 16:32], rows13_v[:, 16:32])
        gated_store(2, 0)
        quantize_h(1, 3 * CHUNK, CHUNK)
        third_product(3, 1, (2, 3))
        gated_store(2, 1)
        gated_store(3, 0)
        gated_store(3, 1, step=1)
